import numpy as np
import ml_dtypes


def mxq(x, axis, fmt="e4m3"):
    dtype, down = {"e4m3": (ml_dtypes.float8_e4m3fn, 7), "e5m2": (ml_dtypes.float8_e5m2, 14)}[fmt]
    v = np.moveaxis(np.asarray(x, np.float32).astype(ml_dtypes.bfloat16).astype(np.float64), axis, -1)
    blocks = v.reshape(v.shape[:-1] + (-1, 32))
    amax = np.abs(blocks).max(-1, keepdims=True)
    byte = np.maximum(np.where(amax > 0, np.frexp(amax)[1] - 1 + 127, 0) - down, 1)
    scale = np.exp2(byte - 127.0)
    codes = (blocks / scale).astype(np.float32).astype(dtype).astype(np.float64)
    return np.moveaxis((codes * scale).reshape(v.shape), -1, axis)


WIDE = False


def mx_kscale(k):
    if not WIDE:
        return np.ones(k)
    levels = np.array([10, -10, 5, -5, 0])
    if k % 512:
        return np.exp2(np.random.permutation(np.resize(levels, k // 32))).repeat(32)
    a = np.empty((k // 512, 16))
    for p in range(k // 512):
        a[p, :8] = np.random.permutation(np.resize(levels, 8))
        for g in range(8):
            far = levels[np.abs(levels - a[p, g]) >= 10]
            a[p, g + 8] = far[np.random.randint(len(far))]
    return np.exp2(a.ravel()).repeat(32)


def f64(x):
    return np.asarray(x).astype(np.float64)


def striped(idx):
    return np.tile(idx.reshape(-1, 16).T, (8, 1)).astype(np.uint16)


def unstriped(offs):
    return offs[:16].T.reshape(-1).astype(np.int64)


E2M1 = np.array([0.0, 0.5, 1.0, 1.5, 2.0, 3.0, 4.0, 6.0, -0.0, -0.5, -1.0, -1.5, -2.0, -3.0, -4.0, -6.0])


def pack_weight(w, fmt):
    k, n = w.shape
    w = f64(np.asarray(w, np.float32).astype(ml_dtypes.bfloat16)).reshape(k // 32, 32, n)
    amax = np.abs(w).max(1)
    if fmt == "e4m3":
        byte = np.frexp(amax)[1] - 1 + 127 - 7
    else:
        mant, ex = np.frexp(amax / 6.0)
        byte = np.where(mant > 0.5, ex, ex - 1) + 127
    byte = np.clip(np.where(amax > 0, byte, 1), 1, 254)
    scaled = (w * np.exp2(127.0 - byte)[:, None, :]).reshape(k, n).astype(np.float32)
    by_word = np.ascontiguousarray(scaled.reshape(k // 512, 128, 4, n).transpose(0, 1, 3, 2))
    if fmt == "e4m3":
        words = by_word.astype(ml_dtypes.float8_e4m3fn).view(np.uint8)
    else:
        c = by_word.astype(ml_dtypes.float4_e2m1fn).view(np.uint8) & 0xF
        words = (c[..., 0::2] | (c[..., 1::2] << 4)).reshape(k // 512, 128, 2 * n)
    return np.ascontiguousarray(words), np.ascontiguousarray(byte.astype(np.uint8).reshape(k // 512, 16, n))


def unpack_weight(words, scales, fmt):
    g, _, n = scales.shape
    words = np.ascontiguousarray(words).reshape(g, 128, n, -1)
    if fmt == "e4m3":
        vals = words.view(ml_dtypes.float8_e4m3fn).astype(np.float64)
    else:
        nib = np.empty((g, 128, n, 4), np.uint8)
        nib[..., 0::2] = words & 0xF
        nib[..., 1::2] = words >> 4
        vals = E2M1[nib]
    vals = vals * np.repeat(np.exp2(scales.astype(np.float64) - 127.0), 8, axis=1)[..., None]
    return vals.transpose(0, 1, 3, 2).reshape(g * 512, n)


def silu(v):
    return v / (1.0 + np.exp(-np.maximum(v, -700.0)))


K, T, E, C, H, N = 1024, 768, 6, 256, 512, 128


def by_expert(wq, xq):
    return np.concatenate([wq[e].T @ xq[:, e * C:(e + 1) * C] for e in range(E)], axis=1)


def setup_inputs():
    n = np.random.standard_normal
    s = mx_kscale(K)[:, None]
    u = mx_kscale(H)
    first = np.random.permutation(np.repeat(np.arange(E), T // E))
    second = (first + 1 + np.random.permutation(np.repeat(np.arange(E - 1), -(-T // (E - 1)))[:T])) % E
    while np.bincount(second, minlength=E).max() != T // E:
        load = np.bincount(second, minlength=E); hi, lo = int(load.argmax()), int(load.argmin())
        t = np.flatnonzero((second == hi) & (first != lo))[0]; second[t] = lo
    slot_token = np.empty(E * C, np.int64); pos = np.empty((2, T), np.int64); fill = np.zeros(E, np.int64)
    place = np.stack([np.random.permutation(C) for _ in range(E)])
    for r, deal in enumerate((first, second)):
        for t in np.random.permutation(T):
            e = deal[t]; j = e * C + place[e, fill[e]]; fill[e] += 1; slot_token[j] = t; pos[r, t] = j
    g = np.random.uniform(0.2, 0.8, T)
    w1 = [pack_weight(m, "e2m1") for m in n((E, K, H)) / np.sqrt(K) / s[None]]
    w3 = [pack_weight(m, "e2m1") for m in n((E, K, H)) / np.sqrt(K) / s[None] * u[None, None, :]]
    w2 = [pack_weight(m, "e2m1") for m in n((E, H, N)) / np.sqrt(H) / u[None, :, None]]
    x = pack_weight(n((K, T)) * s, "e4m3")
    return {
        "x_words": x[0],
        "x_scales": x[1],
        "w1_words": np.stack([m[0] for m in w1]),
        "w1_scales": np.stack([m[1] for m in w1]),
        "w3_words": np.stack([m[0] for m in w3]),
        "w3_scales": np.stack([m[1] for m in w3]),
        "w2_words": np.stack([m[0] for m in w2]),
        "w2_scales": np.stack([m[1] for m in w2]),
        "gate": np.stack([np.tile(g, (N, 1)), np.tile(1.0 - g, (N, 1))]).astype(np.float32),
        "offs": striped(slot_token),
        "pos1": striped(pos[0]),
        "pos2": striped(pos[1]),
    }


def reference(x_words, x_scales, w1_words, w1_scales, w3_words, w3_scales, w2_words, w2_scales, gate, offs, pos1, pos2):
    idx = unstriped(offs)
    w1 = np.stack([unpack_weight(w1_words[e], w1_scales[e], "e2m1") for e in range(E)])
    w3 = np.stack([unpack_weight(w3_words[e], w3_scales[e], "e2m1") for e in range(E)])
    w2 = np.stack([unpack_weight(w2_words[e], w2_scales[e], "e2m1") for e in range(E)])
    xq = unpack_weight(x_words, x_scales, "e4m3")[:, idx]
    h = silu(by_expert(w1, xq))
    h = h * by_expert(w3, xq)
    y = by_expert(w2, mxq(h, 0, "e4m3"))
    return f64(gate[0]) * y[:, unstriped(pos1)] + f64(gate[1]) * y[:, unstriped(pos2)]

@@ -1,0 +1,270 @@
+from contextlib import ExitStack
+
+import concourse.mybir as mybir
+from concourse.masks import make_identity
+
+K, T, E, C, H, N = 1024, 768, 6, 256, 512, 128
+S = E * C
+FLOPS = 2 * S * (2 * K * H + H * N)
+
+F32 = mybir.dt.float32
+BF16 = mybir.dt.bfloat16
+I32 = mybir.dt.int32
+U32 = mybir.dt.uint32
+U16 = mybir.dt.uint16
+U8 = mybir.dt.uint8
+FP8X4 = mybir.dt.float8_e4m3fn_x4
+FP4X4 = mybir.dt.float4_e2m1fn_x4
+MULT = mybir.AluOpType.mult
+ADD = mybir.AluOpType.add
+SILU = mybir.ActivationFunctionType.Silu
+
+P = 128
+PASSES = 2
+TILE = 128
+LIST = 16
+SCALE_GROUPS = ((0, 2), (2, 6))
+BYTE_CHUNKS = ((0, 1), (1, 3), (3, 6))
+OUT_CHUNKS = ((0, 320), (320, 640), (640, 768))
+
+
+def tile_moe_pkd_glu_silu_kernel(
+    tc, x_words, x_scales, w1_words, w1_scales, w3_words, w3_scales, w2_words, w2_scales, gate, offs, pos1, pos2, out
+):
+    nc = tc.nc
+    with ExitStack() as ctx:
+        keep = ctx.enter_context(tc.tile_pool(name="keep", bufs=1))
+        ring = ctx.enter_context(tc.tile_pool(name="ring", bufs=3))
+        psum = ctx.enter_context(tc.psum_pool(name="psum", bufs=1))
+
+        def held(shape, dtype, name):
+            return keep.tile(shape, dtype, name=name, align_bytes=64)
+
+        def zero(engine, tile_ap):
+            engine.memset(tile_ap.bitcast(I32), 0)
+
+        offs_sb = held([P, S // LIST], U16, "offs_sb")
+        pos1_sb = held([P, T // LIST], U16, "pos1_sb")
+        pos2_sb = held([P, T // LIST], U16, "pos2_sb")
+        xs_win = held([P, T], U8, "xs_win")
+        xw_win = [held([P, T], I32, f"xw_win{o}") for o in range(PASSES)]
+        w1_sb = {}
+        w3_sb = {}
+        gate_sb = {}
+        w2_sb = held([P, E * 2 * N], U8, "w2_sb")
+        w1_pl = [held([P, (hi - lo) * PASSES * H], U8, f"w1_pl{lo}") for lo, hi in SCALE_GROUPS]
+        w3_pl = [held([P, (hi - lo) * PASSES * H], U8, f"w3_pl{lo}") for lo, hi in SCALE_GROUPS]
+        w2_pl = held([P, E * N], U8, "w2_pl")
+        xg = [[held([P, C], U32, f"xg{e}_{o}") for o in range(PASSES)] for e in range(E)]
+        xs_both = [held([P, (hi - lo) * C], U8, f"xs_both{lo}") for lo, hi in BYTE_CHUNKS]
+        xs_second = [held([P, (hi - lo) * C], U8, f"xs_second{lo}") for lo, hi in BYTE_CHUNKS]
+        y_sb = held([P, S], F32, "y_sb")
+        ident = held([P, P], F32, "ident")
+
+        up_banks = [psum.tile([P, H], F32, name=f"up_bank{b}") for b in range(6)]
+        turn_bank = psum.tile([P, 512], F32, name="turn_bank")
+        y_bank = psum.tile([P, 512], F32, name="y_bank")
+
+        def load_plane(queue, plane, scales, lo, hi):
+            width = scales.shape[3]
+            for q in range(4):
+                queue.dma_start(
+                    out=plane[32 * q : 32 * q + 4, :].bitcast(I32).rearrange("r (g i) -> r g i", i=width // 4),
+                    in_=scales[lo:hi, :, 4 * q : 4 * q + 4, :].rearrange("e s r i -> r (e s) i").bitcast(I32),
+                )
+
+        def load_words(dst, words, e, tag):
+            dst[e] = ring.tile([P, PASSES * 2 * H], U8, name=f"{tag}{e}", tag=tag, align_bytes=64)
+            nc.sync.dma_start(
+                out=dst[e][:].bitcast(I32).rearrange("p (s b) -> p s b", s=PASSES),
+                in_=words[e].rearrange("s p b -> p s b").bitcast(I32),
+            )
+
+        def load_tokens(o):
+            nc.sync.dma_start(out=xw_win[o][:], in_=x_words[o].rearrange("p t r -> p (t r)").bitcast(I32))
+
+        def load_expert(e):
+            load_words(w1_sb, w1_words, e, "w1_sb")
+            load_words(w3_sb, w3_words, e, "w3_sb")
+
+        def load_gate(r, tag):
+            gate_sb[r] = ring.tile([P, T], F32, name=f"gate_sb{r}", tag=tag, align_bytes=64)
+            nc.sync.dma_start(out=gate_sb[r][:], in_=gate[r])
+
+        zero(nc.gpsimd, xs_win[:])
+        zero(nc.gpsimd, w1_pl[0][:])
+        zero(nc.vector, w3_pl[0][:])
+        zero(nc.vector, xs_second[0][:])
+        zero(nc.vector, w1_pl[1][:])
+        zero(nc.vector, w3_pl[1][:])
+        zero(nc.vector, xs_second[1][:])
+        zero(nc.vector, xs_second[2][:])
+        zero(nc.vector, w2_pl[:])
+
+        nc.sync.dma_start(offs_sb[:], offs)
+        nc.sync.dma_start(pos1_sb[:], pos1)
+        nc.sync.dma_start(pos2_sb[:], pos2)
+        for q in range(4):
+            nc.sync.dma_start(
+                out=xs_win[32 * q : 32 * q + 8, :].bitcast(I32), in_=x_scales[:, 4 * q : 4 * q + 4, :].bitcast(I32)
+            )
+        load_tokens(0)
+        load_plane(nc.sync, w1_pl[0], w1_scales, *SCALE_GROUPS[0])
+        load_words(w1_sb, w1_words, 0, "w1_sb")
+        load_tokens(1)
+        load_plane(nc.sync, w3_pl[0], w3_scales, *SCALE_GROUPS[0])
+        load_words(w3_sb, w3_words, 0, "w3_sb")
+        make_identity(nc, ident[:])
+        load_expert(1)
+        load_plane(nc.sync, w1_pl[1], w1_scales, *SCALE_GROUPS[1])
+        load_plane(nc.sync, w3_pl[1], w3_scales, *SCALE_GROUPS[1])
+        load_expert(2)
+        load_plane(nc.sync, w2_pl, w2_scales, 0, E)
+        nc.sync.dma_start(
+            out=w2_sb[:].bitcast(I32).rearrange("p (e b) -> p e b", e=E),
+            in_=w2_words.rearrange("e s p b -> p (e s) b").bitcast(I32),
+        )
+
+        def slots(lo, hi):
+            return offs_sb[:, lo // LIST : hi // LIST]
+
+        def gather_bytes(c, queue):
+            lo, hi = BYTE_CHUNKS[c]
+            for e0 in range(lo, hi, 2):
+                e1 = min(e0 + 2, hi)
+                nc.vector.tensor_copy(
+                    xs_both[c][:, (e0 - lo) * C : (e1 - lo) * C], xs_win[:].indirect(slots(e0 * C, e1 * C))
+                )
+            queue.dma_start(out=xs_second[c][0:112, :].bitcast(I32), in_=xs_both[c][4:116, :].bitcast(I32))
+
+        def gather_words(e, o, lo, hi):
+            nc.vector.tensor_copy(xg[e][o][:, lo:hi], xw_win[o][:].bitcast(U32).indirect(slots(e * C + lo, e * C + hi)))
+
+        def token_scales(e, o, j):
+            c = [i for i, (lo, hi) in enumerate(BYTE_CHUNKS) if lo <= e < hi][0]
+            col = (e - BYTE_CHUNKS[c][0]) * C + j * TILE
+            return (xs_both, xs_second)[o][c][:, col : col + TILE]
+
+        def up_pass(g, m, o):
+            e, j = divmod(g, 2)
+            grp = [i for i, (lo, hi) in enumerate(SCALE_GROUPS) if lo <= e < hi][0]
+            col = ((e - SCALE_GROUPS[grp][0]) * PASSES + o) * H
+            nc.tensor.matmul_mx(
+                out=up_banks[2 * (g % 3) + m][:],
+                lhsT=xg[e][o][:, j * TILE : (j + 1) * TILE].bitcast(FP8X4),
+                lhsT_scale=token_scales(e, o, j),
+                rhs=(w1_sb, w3_sb)[m][e][:, o * 2 * H : (o + 1) * 2 * H].bitcast(FP4X4),
+                rhs_scale=(w1_pl, w3_pl)[m][grp][:, col : col + H],
+                start=(o == 0),
+                stop=(o == PASSES - 1),
+            )
+
+        def by_word_half(bank):
+            return bank[:].rearrange("s (p u d) -> s u p d", u=2, d=2)
+
+        h_tiles = {}
+
+        def gated(g):
+            act = ring.tile([P, H], F32, name="act", align_bytes=64)
+            nc.scalar.activation(
+                act[:].rearrange("s (u p d) -> s u p d", u=2, d=2), by_word_half(up_banks[2 * (g % 3)]), SILU
+            )
+            h = ring.tile([P, H], BF16, name="h", bufs=4, align_bytes=64)
+            nc.vector.tensor_tensor(
+                h[:].rearrange("s (u p d) -> s u p d", u=2, d=2),
+                by_word_half(up_banks[2 * (g % 3) + 1]),
+                act[:].rearrange("s (u p d) -> s u p d", u=2, d=2),
+                MULT,
+            )
+            h_tiles[g] = h
+
+        packed = {}
+
+        def turn(tiles, bank):
+            width = len(tiles) * TILE
+            for j, g in enumerate(tiles):
+                words = h_tiles[g][:].bitcast(F32)
+                for u in range(2):
+                    col = (2 * j + u) * TILE
+                    nc.tensor.transpose(bank[:, col : col + TILE], words[:, u * P : (u + 1) * P], ident[:])
+            h_turned = ring.tile([P, 4 * C], BF16, name="h_turned", bufs=2, align_bytes=64)
+            nc.scalar.copy(
+                h_turned[:, : 4 * width].bitcast(F32).rearrange("p (j s u) -> p j s u", u=2, s=TILE),
+                bank[:, : 2 * width].rearrange("p (j u s) -> p j s u", u=2, s=TILE),
+            )
+            codes = ring.tile([P, C], U32, name="codes", bufs=2, align_bytes=64)
+            h_scales = ring.tile([P, C], U8, name="h_scales", bufs=2, align_bytes=64)
+            nc.vector.quantize_mx(
+                out=codes[:, :width].bitcast(FP8X4), scales=h_scales[:, :width], in_=h_turned[:, : 4 * width]
+            )
+            packed[tiles[0]] = (codes, h_scales, width)
+
+        def down(g, bank_cols):
+            codes, h_scales, width = packed[g]
+            e = g // 2
+            nc.tensor.matmul_mx(
+                out=bank_cols,
+                lhsT=w2_sb[:, e * 2 * N : (e + 1) * 2 * N].bitcast(FP4X4),
+                lhsT_scale=w2_pl[:, e * N : (e + 1) * N],
+                rhs=codes[:, :width].bitcast(FP8X4),
+                rhs_scale=h_scales[:, :width],
+                start=True,
+                stop=True,
+            )
+            nc.scalar.copy(y_sb[:, g * TILE : g * TILE + width], bank_cols)
+
+        gather_bytes(0, nc.scalar)
+        for o in range(PASSES):
+            for j in range(2):
+                gather_words(0, o, j * TILE, (j + 1) * TILE)
+        gather_bytes(1, nc.scalar)
+        for o in range(PASSES):
+            gather_words(1, o, 0, C)
+        for o in range(PASSES):
+            for m in range(2):
+                for g in range(2):
+                    up_pass(g, m, o)
+        gated(0)
+        gated(1)
+
+        for e in range(1, E):
+            if e == 1:
+                gather_bytes(2, nc.scalar)
+            if e + 2 < E:
+                load_expert(e + 2)
+            elif e + 2 == E:
+                load_gate(0, "w1_sb")
+                load_gate(1, "w3_sb")
+            for j in range(2):
+                g = 2 * e + j
+                for m in range(2):
+                    for o in range(PASSES):
+                        up_pass(g, m, o)
+                gated(g)
+                if e + 1 < E:
+                    gather_words(e + 1, j, 0, C)
+                if j == 0:
+                    if e >= 2:
+                        down(2 * (e - 2), y_bank[:, (e % 2) * C : (e % 2 + 1) * C])
+                    turn([2 * (e - 1), 2 * (e - 1) + 1], turn_bank)
+
+        last = 2 * (E - 1)
+        down(last - 2, y_bank[:, :C])
+        turn([last], turn_bank)
+        turn([last + 1], up_banks[0])
+        down(last, y_bank[:, C : C + TILE])
+        down(last + 1, up_banks[1][:, :TILE])
+
+        for lo, hi in OUT_CHUNKS:
+            first = ring.tile([P, 320], F32, name="first")
+            second = ring.tile([P, 320], F32, name="second")
+            total = ring.tile([P, 320], F32, name="total")
+            n = hi - lo
+            nc.vector.tensor_tensor(
+                first[:, :n], y_sb[:].indirect(pos1_sb[:, lo // LIST : hi // LIST]), gate_sb[0][:, lo:hi], MULT
+            )
+            nc.vector.tensor_tensor(
+                second[:, :n], y_sb[:].indirect(pos2_sb[:, lo // LIST : hi // LIST]), gate_sb[1][:, lo:hi], MULT
+            )
+            nc.vector.tensor_tensor(total[:, :n], first[:, :n], second[:, :n], ADD)
+            nc.sync.dma_start(out=out[:, lo:hi], in_=total[:, :n])

@@ -24,7 +24,7 @@ PASSES = 2
 TILE = 128
 LIST = 16
 SCALE_GROUPS = ((0, 2), (2, 6))
-BYTE_CHUNKS = ((0, 1), (1, 3), (3, 6))
+BYTE_CHUNKS = ((0, 2), (2, 4), (4, 6))
 OUT_CHUNKS = ((0, 320), (320, 640), (640, 768))
 
 
@@ -48,22 +48,23 @@ def tile_moe_pkd_glu_silu_kernel(
         pos2_sb = held([P, T // LIST], U16, "pos2_sb")
         xs_win = held([P, T], U8, "xs_win")
         xw_win = [held([P, T], I32, f"xw_win{o}") for o in range(PASSES)]
-        w1_sb = {}
-        w3_sb = {}
-        gate_sb = {}
+        w1_sb = [held([P, PASSES * 2 * H], U8, f"w1_sb{e}") for e in range(E)]
+        w3_sb = [held([P, PASSES * 2 * H], U8, f"w3_sb{e}") for e in range(E)]
         w2_sb = held([P, E * 2 * N], U8, "w2_sb")
         w1_pl = [held([P, (hi - lo) * PASSES * H], U8, f"w1_pl{lo}") for lo, hi in SCALE_GROUPS]
         w3_pl = [held([P, (hi - lo) * PASSES * H], U8, f"w3_pl{lo}") for lo, hi in SCALE_GROUPS]
         w2_pl = held([P, E * N], U8, "w2_pl")
-        xg = [[held([P, C], U32, f"xg{e}_{o}") for o in range(PASSES)] for e in range(E)]
-        xs_both = [held([P, (hi - lo) * C], U8, f"xs_both{lo}") for lo, hi in BYTE_CHUNKS]
+        gate_sb = [held([P, T], F32, f"gate_sb{r}") for r in range(2)]
+        xg = {}
+        xs_both = {}
         xs_second = [held([P, (hi - lo) * C], U8, f"xs_second{lo}") for lo, hi in BYTE_CHUNKS]
         y_sb = held([P, S], F32, "y_sb")
         ident = held([P, P], F32, "ident")
 
-        up_banks = [psum.tile([P, H], F32, name=f"up_bank{b}") for b in range(6)]
-        turn_bank = psum.tile([P, 512], F32, name="turn_bank")
-        y_bank = psum.tile([P, 512], F32, name="y_bank")
+        banks = [psum.tile([P, H], F32, name=f"bank{b}") for b in range(8)]
+
+        def up_bank(g, m):
+            return banks[2 * (g % 4) + m]
 
         def load_plane(queue, plane, scales, lo, hi):
             width = scales.shape[3]
@@ -73,63 +74,66 @@ def tile_moe_pkd_glu_silu_kernel(
                     in_=scales[lo:hi, :, 4 * q : 4 * q + 4, :].rearrange("e s r i -> r (e s) i").bitcast(I32),
                 )
 
-        def load_words(dst, words, e, tag):
-            dst[e] = ring.tile([P, PASSES * 2 * H], U8, name=f"{tag}{e}", tag=tag, align_bytes=64)
+        def load_words(dst, words, e):
             nc.sync.dma_start(
-                out=dst[e][:].bitcast(I32).rearrange("p (s b) -> p s b", s=PASSES),
+                out=dst[:].bitcast(I32).rearrange("p (s b) -> p s b", s=PASSES),
                 in_=words[e].rearrange("s p b -> p s b").bitcast(I32),
             )
 
         def load_tokens(o):
             nc.sync.dma_start(out=xw_win[o][:], in_=x_words[o].rearrange("p t r -> p (t r)").bitcast(I32))
 
-        def load_expert(e):
-            load_words(w1_sb, w1_words, e, "w1_sb")
-            load_words(w3_sb, w3_words, e, "w3_sb")
-
-        def load_gate(r, tag):
-            gate_sb[r] = ring.tile([P, T], F32, name=f"gate_sb{r}", tag=tag, align_bytes=64)
-            nc.sync.dma_start(out=gate_sb[r][:], in_=gate[r])
-
+        warm_in = held([P, 1], F32, "warm_in")
+        warm_out = held([P, 1], F32, "warm_out")
         zero(nc.gpsimd, xs_win[:])
-        zero(nc.gpsimd, w1_pl[0][:])
+        nc.gpsimd.memset(warm_in[:], 0.0)
+        nc.scalar.activation(warm_out[:], warm_in[:], SILU)
+        zero(nc.vector, w1_pl[0][:])
         zero(nc.vector, w3_pl[0][:])
-        zero(nc.vector, xs_second[0][:])
         zero(nc.vector, w1_pl[1][:])
-        zero(nc.vector, w3_pl[1][:])
-        zero(nc.vector, xs_second[1][:])
-        zero(nc.vector, xs_second[2][:])
-        zero(nc.vector, w2_pl[:])
+        zero(nc.gpsimd, xs_second[0][:])
+        zero(nc.gpsimd, xs_second[1][:])
+        zero(nc.gpsimd, w3_pl[1][:])
+        zero(nc.gpsimd, w2_pl[:])
+        zero(nc.gpsimd, xs_second[2][:])
+        make_identity(nc, ident[:])
 
         nc.sync.dma_start(offs_sb[:], offs)
-        nc.sync.dma_start(pos1_sb[:], pos1)
-        nc.sync.dma_start(pos2_sb[:], pos2)
         for q in range(4):
             nc.sync.dma_start(
                 out=xs_win[32 * q : 32 * q + 8, :].bitcast(I32), in_=x_scales[:, 4 * q : 4 * q + 4, :].bitcast(I32)
             )
         load_tokens(0)
-        load_plane(nc.sync, w1_pl[0], w1_scales, *SCALE_GROUPS[0])
-        load_words(w1_sb, w1_words, 0, "w1_sb")
         load_tokens(1)
+        load_words(w1_sb[0], w1_words, 0)
+        load_plane(nc.sync, w1_pl[0], w1_scales, *SCALE_GROUPS[0])
+        load_words(w3_sb[0], w3_words, 0)
         load_plane(nc.sync, w3_pl[0], w3_scales, *SCALE_GROUPS[0])
-        load_words(w3_sb, w3_words, 0, "w3_sb")
-        make_identity(nc, ident[:])
-        load_expert(1)
+        load_words(w1_sb[1], w1_words, 1)
+        load_words(w3_sb[1], w3_words, 1)
         load_plane(nc.sync, w1_pl[1], w1_scales, *SCALE_GROUPS[1])
         load_plane(nc.sync, w3_pl[1], w3_scales, *SCALE_GROUPS[1])
-        load_expert(2)
+        load_words(w1_sb[2], w1_words, 2)
+        load_words(w3_sb[2], w3_words, 2)
         load_plane(nc.sync, w2_pl, w2_scales, 0, E)
         nc.sync.dma_start(
             out=w2_sb[:].bitcast(I32).rearrange("p (e b) -> p e b", e=E),
             in_=w2_words.rearrange("e s p b -> p (e s) b").bitcast(I32),
         )
+        for e in range(3, E):
+            load_words(w1_sb[e], w1_words, e)
+            load_words(w3_sb[e], w3_words, e)
+        nc.sync.dma_start(pos1_sb[:], pos1)
+        nc.sync.dma_start(pos2_sb[:], pos2)
+        for r in range(2):
+            nc.sync.dma_start(out=gate_sb[r][:], in_=gate[r])
 
         def slots(lo, hi):
             return offs_sb[:, lo // LIST : hi // LIST]
 
         def gather_bytes(c, queue):
             lo, hi = BYTE_CHUNKS[c]
+            xs_both[c] = ring.tile([P, 2 * C], U8, name=f"xs_both{c}", tag="xs_both", bufs=2, align_bytes=64)
             for e0 in range(lo, hi, 2):
                 e1 = min(e0 + 2, hi)
                 nc.vector.tensor_copy(
@@ -138,6 +142,8 @@ def tile_moe_pkd_glu_silu_kernel(
             queue.dma_start(out=xs_second[c][0:112, :].bitcast(I32), in_=xs_both[c][4:116, :].bitcast(I32))
 
         def gather_words(e, o, lo, hi):
+            if lo == 0:
+                xg.setdefault(e, {})[o] = ring.tile([P, C], U32, name=f"xg{e}_{o}", tag=f"xg{o}", bufs=3, align_bytes=64)
             nc.vector.tensor_copy(xg[e][o][:, lo:hi], xw_win[o][:].bitcast(U32).indirect(slots(e * C + lo, e * C + hi)))
 
         def token_scales(e, o, j):
@@ -150,7 +156,7 @@ def tile_moe_pkd_glu_silu_kernel(
             grp = [i for i, (lo, hi) in enumerate(SCALE_GROUPS) if lo <= e < hi][0]
             col = ((e - SCALE_GROUPS[grp][0]) * PASSES + o) * H
             nc.tensor.matmul_mx(
-                out=up_banks[2 * (g % 3) + m][:],
+                out=up_bank(g, m)[:],
                 lhsT=xg[e][o][:, j * TILE : (j + 1) * TILE].bitcast(FP8X4),
                 lhsT_scale=token_scales(e, o, j),
                 rhs=(w1_sb, w3_sb)[m][e][:, o * 2 * H : (o + 1) * 2 * H].bitcast(FP4X4),
@@ -167,12 +173,12 @@ def tile_moe_pkd_glu_silu_kernel(
         def gated(g):
             act = ring.tile([P, H], F32, name="act", align_bytes=64)
             nc.scalar.activation(
-                act[:].rearrange("s (u p d) -> s u p d", u=2, d=2), by_word_half(up_banks[2 * (g % 3)]), SILU
+                act[:].rearrange("s (u p d) -> s u p d", u=2, d=2), by_word_half(up_bank(g, 0)), SILU
             )
             h = ring.tile([P, H], BF16, name="h", bufs=4, align_bytes=64)
             nc.vector.tensor_tensor(
                 h[:].rearrange("s (u p d) -> s u p d", u=2, d=2),
-                by_word_half(up_banks[2 * (g % 3) + 1]),
+                by_word_half(up_bank(g, 1)),
                 act[:].rearrange("s (u p d) -> s u p d", u=2, d=2),
                 MULT,
             )
@@ -213,58 +219,60 @@ def tile_moe_pkd_glu_silu_kernel(
             )
             nc.scalar.copy(y_sb[:, g * TILE : g * TILE + width], bank_cols)
 
-        gather_bytes(0, nc.scalar)
-        for o in range(PASSES):
-            for j in range(2):
-                gather_words(0, o, j * TILE, (j + 1) * TILE)
-        gather_bytes(1, nc.scalar)
+        gather_bytes(0, nc.gpsimd)
+        for j in range(2):
+            gather_words(0, 0, j * TILE, (j + 1) * TILE)
+        for j in range(2):
+            gather_words(0, 1, j * TILE, (j + 1) * TILE)
         for o in range(PASSES):
             gather_words(1, o, 0, C)
+        gather_bytes(1, nc.gpsimd)
         for o in range(PASSES):
+            gather_words(2, o, 0, C)
+        for m in range(2):
+            for g in range(2):
+                up_pass(g, m, 0)
+        for g in range(2):
             for m in range(2):
-                for g in range(2):
-                    up_pass(g, m, o)
+                up_pass(g, m, 1)
         gated(0)
         gated(1)
 
         for e in range(1, E):
-            if e == 1:
-                gather_bytes(2, nc.scalar)
-            if e + 2 < E:
-                load_expert(e + 2)
-            elif e + 2 == E:
-                load_gate(0, "w1_sb")
-                load_gate(1, "w3_sb")
             for j in range(2):
                 g = 2 * e + j
                 for m in range(2):
                     for o in range(PASSES):
                         up_pass(g, m, o)
+                if e + 2 < E:
+                    gather_words(e + 2, j, 0, C)
+                if g == 4:
+                    gather_bytes(2, nc.gpsimd)
                 gated(g)
-                if e + 1 < E:
-                    gather_words(e + 1, j, 0, C)
                 if j == 0:
-                    if e >= 2:
-                        down(2 * (e - 2), y_bank[:, (e % 2) * C : (e % 2 + 1) * C])
-                    turn([2 * (e - 1), 2 * (e - 1) + 1], turn_bank)
+                    turn([g - 2, g - 1], up_bank(g, 0))
+                else:
+                    down(g - 3, up_bank(g, 0)[:, :C])
 
         last = 2 * (E - 1)
-        down(last - 2, y_bank[:, :C])
-        turn([last], turn_bank)
-        turn([last + 1], up_banks[0])
-        down(last, y_bank[:, C : C + TILE])
-        down(last + 1, up_banks[1][:, :TILE])
+        turn([last], up_bank(last - 2, 0))
+        turn([last + 1], up_bank(last - 1, 0))
+        down(last, up_bank(last - 2, 1)[:, :TILE])
+        down(last + 1, up_bank(last - 1, 1)[:, :TILE])
 
-        for lo, hi in OUT_CHUNKS:
-            first = ring.tile([P, 320], F32, name="first")
-            second = ring.tile([P, 320], F32, name="second")
+        def weighted(r, lo, hi):
+            part = ring.tile([P, 320], F32, name=f"part{r}")
+            pos_sb = (pos1_sb, pos2_sb)[r]
+            nc.vector.tensor_tensor(
+                part[:, : hi - lo], y_sb[:].indirect(pos_sb[:, lo // LIST : hi // LIST]), gate_sb[r][:, lo:hi], MULT
+            )
+            return part
+
+        first = weighted(0, *OUT_CHUNKS[0])
+        for c, (lo, hi) in enumerate(OUT_CHUNKS):
+            second = weighted(1, lo, hi)
+            ahead = weighted(0, *OUT_CHUNKS[c + 1]) if c + 1 < len(OUT_CHUNKS) else None
             total = ring.tile([P, 320], F32, name="total")
-            n = hi - lo
-            nc.vector.tensor_tensor(
-                first[:, :n], y_sb[:].indirect(pos1_sb[:, lo // LIST : hi // LIST]), gate_sb[0][:, lo:hi], MULT
-            )
-            nc.vector.tensor_tensor(
-                second[:, :n], y_sb[:].indirect(pos2_sb[:, lo // LIST : hi // LIST]), gate_sb[1][:, lo:hi], MULT
-            )
-            nc.vector.tensor_tensor(total[:, :n], first[:, :n], second[:, :n], ADD)
-            nc.sync.dma_start(out=out[:, lo:hi], in_=total[:, :n])
+            nc.vector.tensor_tensor(total[:, : hi - lo], first[:, : hi - lo], second[:, : hi - lo], ADD)
+            nc.sync.dma_start(out=out[:, lo:hi], in_=total[:, : hi - lo])
+            first = ahead

@@ -24,7 +24,7 @@ PASSES = 2
 TILE = 128
 LIST = 16
 SCALE_GROUPS = ((0, 2), (2, 6))
-BYTE_CHUNKS = ((0, 2), (2, 4), (4, 6))
+BYTE_CHUNKS = ((0, 1), (1, 3), (3, 5), (5, 6))
 OUT_CHUNKS = ((0, 320), (320, 640), (640, 768))
 
 
@@ -47,7 +47,7 @@ def tile_moe_pkd_glu_silu_kernel(
         pos1_sb = held([P, T // LIST], U16, "pos1_sb")
         pos2_sb = held([P, T // LIST], U16, "pos2_sb")
         xs_win = held([P, T], U8, "xs_win")
-        xw_win = [held([P, T], I32, f"xw_win{o}") for o in range(PASSES)]
+        xw_win = held([P, PASSES * T], I32, "xw_win")
         w1_sb = [held([P, PASSES * 2 * H], U8, f"w1_sb{e}") for e in range(E)]
         w3_sb = [held([P, PASSES * 2 * H], U8, f"w3_sb{e}") for e in range(E)]
         w2_sb = held([P, E * 2 * N], U8, "w2_sb")
@@ -80,9 +80,6 @@ def tile_moe_pkd_glu_silu_kernel(
                 in_=words[e].rearrange("s p b -> p s b").bitcast(I32),
             )
 
-        def load_tokens(o):
-            nc.sync.dma_start(out=xw_win[o][:], in_=x_words[o].rearrange("p t r -> p (t r)").bitcast(I32))
-
         warm_in = held([P, 1], F32, "warm_in")
         warm_out = held([P, 1], F32, "warm_out")
         zero(nc.gpsimd, xs_win[:])
@@ -96,6 +93,7 @@ def tile_moe_pkd_glu_silu_kernel(
         zero(nc.gpsimd, w3_pl[1][:])
         zero(nc.gpsimd, w2_pl[:])
         zero(nc.gpsimd, xs_second[2][:])
+        zero(nc.gpsimd, xs_second[3][:])
         make_identity(nc, ident[:])
 
         nc.sync.dma_start(offs_sb[:], offs)
@@ -103,8 +101,10 @@ def tile_moe_pkd_glu_silu_kernel(
             nc.sync.dma_start(
                 out=xs_win[32 * q : 32 * q + 8, :].bitcast(I32), in_=x_scales[:, 4 * q : 4 * q + 4, :].bitcast(I32)
             )
-        load_tokens(0)
-        load_tokens(1)
+        nc.sync.dma_start(
+            out=xw_win[:].rearrange("p (o t) -> p o t", o=PASSES),
+            in_=x_words.rearrange("o p t r -> p o (t r)").bitcast(I32),
+        )
         load_words(w1_sb[0], w1_words, 0)
         load_plane(nc.sync, w1_pl[0], w1_scales, *SCALE_GROUPS[0])
         load_words(w3_sb[0], w3_words, 0)
@@ -139,12 +139,15 @@ def tile_moe_pkd_glu_silu_kernel(
                 nc.vector.tensor_copy(
                     xs_both[c][:, (e0 - lo) * C : (e1 - lo) * C], xs_win[:].indirect(slots(e0 * C, e1 * C))
                 )
-            queue.dma_start(out=xs_second[c][0:112, :].bitcast(I32), in_=xs_both[c][4:116, :].bitcast(I32))
+            queue.dma_start(
+                out=xs_second[c][0:112, :].bitcast(I32), in_=xs_both[c][4:116, : (hi - lo) * C].bitcast(I32)
+            )
 
         def gather_words(e, o, lo, hi):
             if lo == 0:
-                xg.setdefault(e, {})[o] = ring.tile([P, C], U32, name=f"xg{e}_{o}", tag=f"xg{o}", bufs=3, align_bytes=64)
-            nc.vector.tensor_copy(xg[e][o][:, lo:hi], xw_win[o][:].bitcast(U32).indirect(slots(e * C + lo, e * C + hi)))
+                xg.setdefault(e, {})[o] = ring.tile([P, C], U32, name=f"xg{e}_{o}", tag=f"xg{o}", bufs=4, align_bytes=64)
+            window = xw_win[:, o * T : (o + 1) * T].bitcast(U32)
+            nc.vector.tensor_copy(xg[e][o][:, lo:hi], window.indirect(slots(e * C + lo, e * C + hi)))
 
         def token_scales(e, o, j):
             c = [i for i, (lo, hi) in enumerate(BYTE_CHUNKS) if lo <= e < hi][0]
@@ -198,8 +201,8 @@ def tile_moe_pkd_glu_silu_kernel(
                 h_turned[:, : 4 * width].bitcast(F32).rearrange("p (j s u) -> p j s u", u=2, s=TILE),
                 bank[:, : 2 * width].rearrange("p (j u s) -> p j s u", u=2, s=TILE),
             )
-            codes = ring.tile([P, C], U32, name="codes", bufs=2, align_bytes=64)
-            h_scales = ring.tile([P, C], U8, name="h_scales", bufs=2, align_bytes=64)
+            codes = ring.tile([P, C], U32, name="codes", bufs=3, align_bytes=64)
+            h_scales = ring.tile([P, C], U8, name="h_scales", bufs=3, align_bytes=64)
             nc.vector.quantize_mx(
                 out=codes[:, :width].bitcast(FP8X4), scales=h_scales[:, :width], in_=h_turned[:, : 4 * width]
             )
@@ -219,22 +222,21 @@ def tile_moe_pkd_glu_silu_kernel(
             )
             nc.scalar.copy(y_sb[:, g * TILE : g * TILE + width], bank_cols)
 
-        gather_bytes(0, nc.gpsimd)
+        gather_bytes(0, nc.scalar)
         for j in range(2):
             gather_words(0, 0, j * TILE, (j + 1) * TILE)
         for j in range(2):
             gather_words(0, 1, j * TILE, (j + 1) * TILE)
-        for o in range(PASSES):
-            gather_words(1, o, 0, C)
         gather_bytes(1, nc.gpsimd)
+        for e in range(1, 4):
+            for o in range(PASSES):
+                gather_words(e, o, 0, C)
         for o in range(PASSES):
-            gather_words(2, o, 0, C)
-        for m in range(2):
             for g in range(2):
-                up_pass(g, m, 0)
+                up_pass(g, 0, o)
         for g in range(2):
-            for m in range(2):
-                up_pass(g, m, 1)
+            for o in range(PASSES):
+                up_pass(g, 1, o)
         gated(0)
         gated(1)
 
@@ -244,21 +246,24 @@ def tile_moe_pkd_glu_silu_kernel(
                 for m in range(2):
                     for o in range(PASSES):
                         up_pass(g, m, o)
-                if e + 2 < E:
-                    gather_words(e + 2, j, 0, C)
-                if g == 4:
-                    gather_bytes(2, nc.gpsimd)
+                if e + 3 < E:
+                    gather_words(e + 3, j, 0, C)
                 gated(g)
-                if j == 0:
-                    turn([g - 2, g - 1], up_bank(g, 0))
-                else:
-                    down(g - 3, up_bank(g, 0)[:, :C])
+                if j == (e == E - 1):
+                    turn([2 * e - 2, 2 * e - 1], up_bank(g, 0))
+                if j == 0 and e >= 2:
+                    down(g - 4, up_bank(g, 1)[:, :C])
+                if g == 3:
+                    gather_bytes(2, nc.gpsimd)
+                if g == 7:
+                    gather_bytes(3, nc.gpsimd)
 
         last = 2 * (E - 1)
         turn([last], up_bank(last - 2, 0))
+        down(last - 2, up_bank(last - 2, 1)[:, :C])
         turn([last + 1], up_bank(last - 1, 0))
-        down(last, up_bank(last - 2, 1)[:, :TILE])
-        down(last + 1, up_bank(last - 1, 1)[:, :TILE])
+        down(last, up_bank(last - 1, 1)[:, :TILE])
+        down(last + 1, up_bank(last, 0)[:, :TILE])
 
         def weighted(r, lo, hi):
             part = ring.tile([P, 320], F32, name=f"part{r}")

@@ -22,10 +22,16 @@ SILU = mybir.ActivationFunctionType.Silu
 P = 128
 PASSES = 2
 TILE = 128
+TILES = S // TILE
 LIST = 16
 SCALE_GROUPS = ((0, 2), (2, 6))
-BYTE_CHUNKS = ((0, 1), (1, 3), (3, 5), (5, 6))
+WORD_GROUPS = (((0, 1), (1, 3), (3, 4), (4, 6)), ((0, 1), (1, 3), (3, 4), (4, 6)))
+BYTE_CHUNKS = ((0, 1), (1, 6))
 OUT_CHUNKS = ((0, 320), (320, 640), (640, 768))
+
+
+def group_of(groups, e):
+    return [i for i, (lo, hi) in enumerate(groups) if lo <= e < hi][0]
 
 
 def tile_moe_pkd_glu_silu_kernel(
@@ -48,15 +54,15 @@ def tile_moe_pkd_glu_silu_kernel(
         pos2_sb = held([P, T // LIST], U16, "pos2_sb")
         xs_win = held([P, T], U8, "xs_win")
         xw_win = held([P, PASSES * T], I32, "xw_win")
-        w1_sb = [held([P, PASSES * 2 * H], U8, f"w1_sb{e}") for e in range(E)]
-        w3_sb = [held([P, PASSES * 2 * H], U8, f"w3_sb{e}") for e in range(E)]
+        w1_sb = [held([P, (hi - lo) * PASSES * 2 * H], U8, f"w1_sb{lo}") for lo, hi in WORD_GROUPS[0]]
+        w3_sb = [held([P, (hi - lo) * PASSES * 2 * H], U8, f"w3_sb{lo}") for lo, hi in WORD_GROUPS[1]]
         w2_sb = held([P, E * 2 * N], U8, "w2_sb")
         w1_pl = [held([P, (hi - lo) * PASSES * H], U8, f"w1_pl{lo}") for lo, hi in SCALE_GROUPS]
         w3_pl = [held([P, (hi - lo) * PASSES * H], U8, f"w3_pl{lo}") for lo, hi in SCALE_GROUPS]
         w2_pl = held([P, E * N], U8, "w2_pl")
-        gate_sb = [held([P, T], F32, f"gate_sb{r}") for r in range(2)]
-        xg = {}
-        xs_both = {}
+        gate_sb = held([P, 2 * T], F32, "gate_sb")
+        xg = [held([P, 3 * C], U32, f"xg{o}") for o in range(PASSES)]
+        xs_both = [held([P, (hi - lo) * C], U8, f"xs_both{lo}") for lo, hi in BYTE_CHUNKS]
         xs_second = [held([P, (hi - lo) * C], U8, f"xs_second{lo}") for lo, hi in BYTE_CHUNKS]
         y_sb = held([P, S], F32, "y_sb")
         ident = held([P, P], F32, "ident")
@@ -74,28 +80,25 @@ def tile_moe_pkd_glu_silu_kernel(
                     in_=scales[lo:hi, :, 4 * q : 4 * q + 4, :].rearrange("e s r i -> r (e s) i").bitcast(I32),
                 )
 
-        def load_words(dst, words, e):
+        def load_words(m, grp):
+            lo, hi = WORD_GROUPS[m][grp]
             nc.sync.dma_start(
-                out=dst[:].bitcast(I32).rearrange("p (s b) -> p s b", s=PASSES),
-                in_=words[e].rearrange("s p b -> p s b").bitcast(I32),
+                out=(w1_sb, w3_sb)[m][grp][:].bitcast(I32).rearrange("p (s b) -> p s b", s=(hi - lo) * PASSES),
+                in_=(w1_words, w3_words)[m][lo:hi].rearrange("e s p b -> p (e s) b").bitcast(I32),
             )
 
-        warm_in = held([P, 1], F32, "warm_in")
-        warm_out = held([P, 1], F32, "warm_out")
         zero(nc.gpsimd, xs_win[:])
-        nc.gpsimd.memset(warm_in[:], 0.0)
-        nc.scalar.activation(warm_out[:], warm_in[:], SILU)
         zero(nc.vector, w1_pl[0][:])
-        zero(nc.vector, w3_pl[0][:])
+        zero(nc.gpsimd, w3_pl[0][:])
+        zero(nc.vector, xs_second[0][:])
+        zero(nc.vector, xs_second[1][:])
         zero(nc.vector, w1_pl[1][:])
-        zero(nc.gpsimd, xs_second[0][:])
-        zero(nc.gpsimd, xs_second[1][:])
         zero(nc.gpsimd, w3_pl[1][:])
-        zero(nc.gpsimd, w2_pl[:])
-        zero(nc.gpsimd, xs_second[2][:])
-        zero(nc.gpsimd, xs_second[3][:])
+        zero(nc.vector, w2_pl[:])
         make_identity(nc, ident[:])
 
+        load_plane(nc.scalar, w1_pl[0], w1_scales, *SCALE_GROUPS[0])
+        load_plane(nc.scalar, w3_pl[0], w3_scales, *SCALE_GROUPS[0])
         nc.sync.dma_start(offs_sb[:], offs)
         for q in range(4):
             nc.sync.dma_start(
@@ -105,64 +108,61 @@ def tile_moe_pkd_glu_silu_kernel(
             out=xw_win[:].rearrange("p (o t) -> p o t", o=PASSES),
             in_=x_words.rearrange("o p t r -> p o (t r)").bitcast(I32),
         )
-        load_words(w1_sb[0], w1_words, 0)
-        load_plane(nc.sync, w1_pl[0], w1_scales, *SCALE_GROUPS[0])
-        load_words(w3_sb[0], w3_words, 0)
-        load_plane(nc.sync, w3_pl[0], w3_scales, *SCALE_GROUPS[0])
-        load_words(w1_sb[1], w1_words, 1)
-        load_words(w3_sb[1], w3_words, 1)
+        load_words(0, 0)
+        load_words(1, 0)
+        load_words(0, 1)
+        load_words(1, 1)
         load_plane(nc.sync, w1_pl[1], w1_scales, *SCALE_GROUPS[1])
         load_plane(nc.sync, w3_pl[1], w3_scales, *SCALE_GROUPS[1])
-        load_words(w1_sb[2], w1_words, 2)
-        load_words(w3_sb[2], w3_words, 2)
+        load_words(0, 2)
+        load_words(1, 2)
         load_plane(nc.sync, w2_pl, w2_scales, 0, E)
         nc.sync.dma_start(
             out=w2_sb[:].bitcast(I32).rearrange("p (e b) -> p e b", e=E),
             in_=w2_words.rearrange("e s p b -> p (e s) b").bitcast(I32),
         )
-        for e in range(3, E):
-            load_words(w1_sb[e], w1_words, e)
-            load_words(w3_sb[e], w3_words, e)
+        load_words(0, 3)
+        load_words(1, 3)
         nc.sync.dma_start(pos1_sb[:], pos1)
         nc.sync.dma_start(pos2_sb[:], pos2)
-        for r in range(2):
-            nc.sync.dma_start(out=gate_sb[r][:], in_=gate[r])
+        nc.sync.dma_start(out=gate_sb[:].rearrange("n (r t) -> n r t", r=2), in_=gate.rearrange("r n t -> n r t"))
 
         def slots(lo, hi):
             return offs_sb[:, lo // LIST : hi // LIST]
 
-        def gather_bytes(c, queue):
+        def gather_bytes(c):
             lo, hi = BYTE_CHUNKS[c]
-            xs_both[c] = ring.tile([P, 2 * C], U8, name=f"xs_both{c}", tag="xs_both", bufs=2, align_bytes=64)
             for e0 in range(lo, hi, 2):
                 e1 = min(e0 + 2, hi)
                 nc.vector.tensor_copy(
                     xs_both[c][:, (e0 - lo) * C : (e1 - lo) * C], xs_win[:].indirect(slots(e0 * C, e1 * C))
                 )
-            queue.dma_start(
-                out=xs_second[c][0:112, :].bitcast(I32), in_=xs_both[c][4:116, : (hi - lo) * C].bitcast(I32)
-            )
+            nc.scalar.dma_start(out=xs_second[c][0:112, :].bitcast(I32), in_=xs_both[c][4:116, :].bitcast(I32))
+
+        def word_col(e):
+            return 0 if e == 0 else (1 + (e - 1) % 2) * C
 
         def gather_words(e, o, lo, hi):
-            if lo == 0:
-                xg.setdefault(e, {})[o] = ring.tile([P, C], U32, name=f"xg{e}_{o}", tag=f"xg{o}", bufs=4, align_bytes=64)
             window = xw_win[:, o * T : (o + 1) * T].bitcast(U32)
-            nc.vector.tensor_copy(xg[e][o][:, lo:hi], window.indirect(slots(e * C + lo, e * C + hi)))
+            col = word_col(e)
+            nc.vector.tensor_copy(xg[o][:, col + lo : col + hi], window.indirect(slots(e * C + lo, e * C + hi)))
 
         def token_scales(e, o, j):
-            c = [i for i, (lo, hi) in enumerate(BYTE_CHUNKS) if lo <= e < hi][0]
+            c = group_of(BYTE_CHUNKS, e)
             col = (e - BYTE_CHUNKS[c][0]) * C + j * TILE
             return (xs_both, xs_second)[o][c][:, col : col + TILE]
 
         def up_pass(g, m, o):
             e, j = divmod(g, 2)
-            grp = [i for i, (lo, hi) in enumerate(SCALE_GROUPS) if lo <= e < hi][0]
+            grp = group_of(SCALE_GROUPS, e)
             col = ((e - SCALE_GROUPS[grp][0]) * PASSES + o) * H
+            wgrp = group_of(WORD_GROUPS[m], e)
+            wcol = ((e - WORD_GROUPS[m][wgrp][0]) * PASSES + o) * 2 * H
             nc.tensor.matmul_mx(
                 out=up_bank(g, m)[:],
-                lhsT=xg[e][o][:, j * TILE : (j + 1) * TILE].bitcast(FP8X4),
+                lhsT=xg[o][:, word_col(e) + j * TILE : word_col(e) + (j + 1) * TILE].bitcast(FP8X4),
                 lhsT_scale=token_scales(e, o, j),
-                rhs=(w1_sb, w3_sb)[m][e][:, o * 2 * H : (o + 1) * 2 * H].bitcast(FP4X4),
+                rhs=(w1_sb, w3_sb)[m][wgrp][:, wcol : wcol + 2 * H].bitcast(FP4X4),
                 rhs_scale=(w1_pl, w3_pl)[m][grp][:, col : col + H],
                 start=(o == 0),
                 stop=(o == PASSES - 1),
@@ -174,11 +174,11 @@ def tile_moe_pkd_glu_silu_kernel(
         h_tiles = {}
 
         def gated(g):
-            act = ring.tile([P, H], F32, name="act", align_bytes=64)
+            act = ring.tile([P, H], F32, name="act", bufs=4, align_bytes=64)
             nc.scalar.activation(
                 act[:].rearrange("s (u p d) -> s u p d", u=2, d=2), by_word_half(up_bank(g, 0)), SILU
             )
-            h = ring.tile([P, H], BF16, name="h", bufs=4, align_bytes=64)
+            h = held([P, H], BF16, f"h{g}")
             nc.vector.tensor_tensor(
                 h[:].rearrange("s (u p d) -> s u p d", u=2, d=2),
                 by_word_half(up_bank(g, 1)),
@@ -196,80 +196,77 @@ def tile_moe_pkd_glu_silu_kernel(
                 for u in range(2):
                     col = (2 * j + u) * TILE
                     nc.tensor.transpose(bank[:, col : col + TILE], words[:, u * P : (u + 1) * P], ident[:])
-            h_turned = ring.tile([P, 4 * C], BF16, name="h_turned", bufs=2, align_bytes=64)
+            h_turned = held([P, 4 * width], BF16, f"h_turned{tiles[0]}")
             nc.scalar.copy(
-                h_turned[:, : 4 * width].bitcast(F32).rearrange("p (j s u) -> p j s u", u=2, s=TILE),
+                h_turned[:].bitcast(F32).rearrange("p (j s u) -> p j s u", u=2, s=TILE),
                 bank[:, : 2 * width].rearrange("p (j u s) -> p j s u", u=2, s=TILE),
             )
-            codes = ring.tile([P, C], U32, name="codes", bufs=3, align_bytes=64)
-            h_scales = ring.tile([P, C], U8, name="h_scales", bufs=3, align_bytes=64)
-            nc.vector.quantize_mx(
-                out=codes[:, :width].bitcast(FP8X4), scales=h_scales[:, :width], in_=h_turned[:, : 4 * width]
-            )
+            codes = held([P, width], U32, f"codes{tiles[0]}")
+            h_scales = held([P, width], U8, f"h_scales{tiles[0]}")
+            nc.vector.quantize_mx(out=codes[:].bitcast(FP8X4), scales=h_scales[:], in_=h_turned[:])
             packed[tiles[0]] = (codes, h_scales, width)
 
-        def down(g, bank_cols):
+        def down(g, bank):
             codes, h_scales, width = packed[g]
             e = g // 2
             nc.tensor.matmul_mx(
-                out=bank_cols,
+                out=bank[:, :width],
                 lhsT=w2_sb[:, e * 2 * N : (e + 1) * 2 * N].bitcast(FP4X4),
                 lhsT_scale=w2_pl[:, e * N : (e + 1) * N],
-                rhs=codes[:, :width].bitcast(FP8X4),
-                rhs_scale=h_scales[:, :width],
+                rhs=codes[:].bitcast(FP8X4),
+                rhs_scale=h_scales[:],
                 start=True,
                 stop=True,
             )
-            nc.scalar.copy(y_sb[:, g * TILE : g * TILE + width], bank_cols)
+            nc.scalar.copy(y_sb[:, g * TILE : g * TILE + width], bank[:, :width])
 
-        gather_bytes(0, nc.scalar)
+        gather_bytes(0)
+        gather_bytes(1)
         for j in range(2):
             gather_words(0, 0, j * TILE, (j + 1) * TILE)
-        for j in range(2):
-            gather_words(0, 1, j * TILE, (j + 1) * TILE)
-        gather_bytes(1, nc.gpsimd)
-        for e in range(1, 4):
+        gather_words(0, 1, 0, C)
+        for e in range(1, 3):
             for o in range(PASSES):
                 gather_words(e, o, 0, C)
         for o in range(PASSES):
             for g in range(2):
                 up_pass(g, 0, o)
-        for g in range(2):
-            for o in range(PASSES):
+        for o in range(PASSES):
+            for g in range(2):
                 up_pass(g, 1, o)
         gated(0)
         gated(1)
 
-        for e in range(1, E):
-            for j in range(2):
-                g = 2 * e + j
-                for m in range(2):
-                    for o in range(PASSES):
-                        up_pass(g, m, o)
-                if e + 3 < E:
-                    gather_words(e + 3, j, 0, C)
-                gated(g)
-                if j == (e == E - 1):
-                    turn([2 * e - 2, 2 * e - 1], up_bank(g, 0))
-                if j == 0 and e >= 2:
-                    down(g - 4, up_bank(g, 1)[:, :C])
-                if g == 3:
-                    gather_bytes(2, nc.gpsimd)
-                if g == 7:
-                    gather_bytes(3, nc.gpsimd)
+        for g in range(2, TILES):
+            e, j = divmod(g, 2)
+            for m in range(2):
+                for o in range(PASSES):
+                    up_pass(g, m, o)
+            gated(g)
+            if 3 <= e + 1 < E:
+                gather_words(e + 1, j, 0, C)
+            if j == 0 and e >= 2:
+                turn([g - 4, g - 3], up_bank(g, 0))
+            if j == 0 and e >= 3:
+                down(g - 6, up_bank(g, 1))
 
-        last = 2 * (E - 1)
-        turn([last], up_bank(last - 2, 0))
-        down(last - 2, up_bank(last - 2, 1)[:, :C])
-        turn([last + 1], up_bank(last - 1, 0))
-        down(last, up_bank(last - 1, 1)[:, :TILE])
-        down(last + 1, up_bank(last, 0)[:, :TILE])
+        last = TILES - 1
+        turn([last - 3, last - 2], up_bank(last, 0))
+        down(last - 5, up_bank(last - 2, 1))
+        turn([last - 1], up_bank(last - 2, 0))
+        down(last - 3, up_bank(last - 3, 1))
+        turn([last], up_bank(last - 3, 0))
+        down(last - 1, up_bank(last - 1, 1))
+        down(last, up_bank(last, 1))
 
         def weighted(r, lo, hi):
             part = ring.tile([P, 320], F32, name=f"part{r}")
             pos_sb = (pos1_sb, pos2_sb)[r]
             nc.vector.tensor_tensor(
-                part[:, : hi - lo], y_sb[:].indirect(pos_sb[:, lo // LIST : hi // LIST]), gate_sb[r][:, lo:hi], MULT
+                part[:, : hi - lo],
+                y_sb[:].indirect(pos_sb[:, lo // LIST : hi // LIST]),
+                gate_sb[:, r * T + lo : r * T + hi],
+                MULT,
             )
             return part
 

@@ -24,9 +24,11 @@ PASSES = 2
 TILE = 128
 TILES = S // TILE
 LIST = 16
-SCALE_GROUPS = ((0, 2), (2, 6))
-WORD_GROUPS = (((0, 1), (1, 3), (3, 4), (4, 6)), ((0, 1), (1, 3), (3, 4), (4, 6)))
+SCALE_GROUPS = ((0, 2), (2, 4), (4, 6))
+WORD_GROUPS = ((0, 1), (1, 2), (2, 3), (3, 4), (4, 6))
 BYTE_CHUNKS = ((0, 1), (1, 6))
+AHEAD = 7
+REUSE = 3
 OUT_CHUNKS = ((0, 320), (320, 640), (640, 768))
 
 
@@ -54,14 +56,14 @@ def tile_moe_pkd_glu_silu_kernel(
         pos2_sb = held([P, T // LIST], U16, "pos2_sb")
         xs_win = held([P, T], U8, "xs_win")
         xw_win = held([P, PASSES * T], I32, "xw_win")
-        w1_sb = [held([P, (hi - lo) * PASSES * 2 * H], U8, f"w1_sb{lo}") for lo, hi in WORD_GROUPS[0]]
-        w3_sb = [held([P, (hi - lo) * PASSES * 2 * H], U8, f"w3_sb{lo}") for lo, hi in WORD_GROUPS[1]]
+        w1_sb = [held([P, (hi - lo) * PASSES * 2 * H], U8, f"w1_sb{lo}") for lo, hi in WORD_GROUPS]
+        w3_sb = [held([P, (hi - lo) * PASSES * 2 * H], U8, f"w3_sb{lo}") for lo, hi in WORD_GROUPS]
         w2_sb = held([P, E * 2 * N], U8, "w2_sb")
         w1_pl = [held([P, (hi - lo) * PASSES * H], U8, f"w1_pl{lo}") for lo, hi in SCALE_GROUPS]
         w3_pl = [held([P, (hi - lo) * PASSES * H], U8, f"w3_pl{lo}") for lo, hi in SCALE_GROUPS]
         w2_pl = held([P, E * N], U8, "w2_pl")
         gate_sb = held([P, 2 * T], F32, "gate_sb")
-        xg = [held([P, 3 * C], U32, f"xg{o}") for o in range(PASSES)]
+        xg = [held([P, AHEAD * TILE], U32, f"xg{o}") for o in range(PASSES)]
         xs_both = [held([P, (hi - lo) * C], U8, f"xs_both{lo}") for lo, hi in BYTE_CHUNKS]
         xs_second = [held([P, (hi - lo) * C], U8, f"xs_second{lo}") for lo, hi in BYTE_CHUNKS]
         y_sb = held([P, S], F32, "y_sb")
@@ -74,55 +76,63 @@ def tile_moe_pkd_glu_silu_kernel(
 
         def load_plane(queue, plane, scales, lo, hi):
             width = scales.shape[3]
-            for q in range(4):
+            rows = scales[lo:hi].rearrange("e s (q r) i -> r q (e s) i", r=4)
+            for r in range(4):
                 queue.dma_start(
-                    out=plane[32 * q : 32 * q + 4, :].bitcast(I32).rearrange("r (g i) -> r g i", i=width // 4),
-                    in_=scales[lo:hi, :, 4 * q : 4 * q + 4, :].rearrange("e s r i -> r (e s) i").bitcast(I32),
+                    out=plane[r:P:32, :].bitcast(I32).rearrange("q (g i) -> q g i", i=width // 4),
+                    in_=rows[r].bitcast(I32),
                 )
 
-        def load_words(m, grp):
-            lo, hi = WORD_GROUPS[m][grp]
-            nc.sync.dma_start(
+        def load_scales(queue, m, grp):
+            load_plane(queue, (w1_pl, w3_pl)[m][grp], (w1_scales, w3_scales)[m], *SCALE_GROUPS[grp])
+
+        def load_words(queue, m, grp):
+            lo, hi = WORD_GROUPS[grp]
+            queue.dma_start(
                 out=(w1_sb, w3_sb)[m][grp][:].bitcast(I32).rearrange("p (s b) -> p s b", s=(hi - lo) * PASSES),
                 in_=(w1_words, w3_words)[m][lo:hi].rearrange("e s p b -> p (e s) b").bitcast(I32),
             )
 
         zero(nc.gpsimd, xs_win[:])
-        zero(nc.vector, w1_pl[0][:])
-        zero(nc.gpsimd, w3_pl[0][:])
-        zero(nc.vector, xs_second[0][:])
         zero(nc.vector, xs_second[1][:])
         zero(nc.vector, w1_pl[1][:])
+        zero(nc.vector, w1_pl[2][:])
+        zero(nc.vector, w1_pl[0][:])
+        zero(nc.vector, w3_pl[0][:])
+        zero(nc.gpsimd, xs_second[0][:])
         zero(nc.gpsimd, w3_pl[1][:])
-        zero(nc.vector, w2_pl[:])
+        zero(nc.gpsimd, w2_pl[:])
+        zero(nc.gpsimd, w3_pl[2][:])
         make_identity(nc, ident[:])
 
-        load_plane(nc.scalar, w1_pl[0], w1_scales, *SCALE_GROUPS[0])
-        load_plane(nc.scalar, w3_pl[0], w3_scales, *SCALE_GROUPS[0])
         nc.sync.dma_start(offs_sb[:], offs)
-        for q in range(4):
-            nc.sync.dma_start(
-                out=xs_win[32 * q : 32 * q + 8, :].bitcast(I32), in_=x_scales[:, 4 * q : 4 * q + 4, :].bitcast(I32)
-            )
+        token_rows = x_scales.rearrange("o (q r) t -> r q o t", r=4)
+        for r in range(4):
+            nc.sync.dma_start(out=xs_win[r:P:16, :].bitcast(I32), in_=token_rows[r].bitcast(I32))
         nc.sync.dma_start(
             out=xw_win[:].rearrange("p (o t) -> p o t", o=PASSES),
             in_=x_words.rearrange("o p t r -> p o (t r)").bitcast(I32),
         )
-        load_words(0, 0)
-        load_words(1, 0)
-        load_words(0, 1)
-        load_words(1, 1)
-        load_plane(nc.sync, w1_pl[1], w1_scales, *SCALE_GROUPS[1])
-        load_plane(nc.sync, w3_pl[1], w3_scales, *SCALE_GROUPS[1])
-        load_words(0, 2)
-        load_words(1, 2)
+        load_words(nc.sync, 0, 0)
+        load_words(nc.sync, 1, 0)
+        load_words(nc.sync, 1, 1)
+        load_words(nc.sync, 0, 1)
+        load_scales(nc.scalar, 0, 0)
+        load_scales(nc.scalar, 1, 0)
+        for m in range(2):
+            load_scales(nc.sync, m, 1)
+        for grp in (2, 3):
+            load_words(nc.sync, 1, grp)
+            load_words(nc.sync, 0, grp)
         load_plane(nc.sync, w2_pl, w2_scales, 0, E)
         nc.sync.dma_start(
             out=w2_sb[:].bitcast(I32).rearrange("p (e b) -> p e b", e=E),
             in_=w2_words.rearrange("e s p b -> p (e s) b").bitcast(I32),
         )
-        load_words(0, 3)
-        load_words(1, 3)
+        for m in range(2):
+            load_scales(nc.sync, m, 2)
+        load_words(nc.sync, 1, 4)
+        load_words(nc.sync, 0, 4)
         nc.sync.dma_start(pos1_sb[:], pos1)
         nc.sync.dma_start(pos2_sb[:], pos2)
         nc.sync.dma_start(out=gate_sb[:].rearrange("n (r t) -> n r t", r=2), in_=gate.rearrange("r n t -> n r t"))
@@ -137,15 +147,17 @@ def tile_moe_pkd_glu_silu_kernel(
                 nc.vector.tensor_copy(
                     xs_both[c][:, (e0 - lo) * C : (e1 - lo) * C], xs_win[:].indirect(slots(e0 * C, e1 * C))
                 )
-            nc.scalar.dma_start(out=xs_second[c][0:112, :].bitcast(I32), in_=xs_both[c][4:116, :].bitcast(I32))
+            nc.scalar.dma_start(out=xs_second[c][0:112, :].bitcast(I32), in_=xs_both[c][16:P, :].bitcast(I32))
 
-        def word_col(e):
-            return 0 if e == 0 else (1 + (e - 1) % 2) * C
+        def word_col(g):
+            return (g if g < AHEAD else AHEAD - REUSE + (g - AHEAD) % REUSE) * TILE
 
-        def gather_words(e, o, lo, hi):
+        def gather_words(o, g0, g1):
             window = xw_win[:, o * T : (o + 1) * T].bitcast(U32)
-            col = word_col(e)
-            nc.vector.tensor_copy(xg[o][:, col + lo : col + hi], window.indirect(slots(e * C + lo, e * C + hi)))
+            col = word_col(g0)
+            nc.vector.tensor_copy(
+                xg[o][:, col : col + (g1 - g0) * TILE], window.indirect(slots(g0 * TILE, g1 * TILE))
+            )
 
         def token_scales(e, o, j):
             c = group_of(BYTE_CHUNKS, e)
@@ -156,11 +168,11 @@ def tile_moe_pkd_glu_silu_kernel(
             e, j = divmod(g, 2)
             grp = group_of(SCALE_GROUPS, e)
             col = ((e - SCALE_GROUPS[grp][0]) * PASSES + o) * H
-            wgrp = group_of(WORD_GROUPS[m], e)
-            wcol = ((e - WORD_GROUPS[m][wgrp][0]) * PASSES + o) * 2 * H
+            wgrp = group_of(WORD_GROUPS, e)
+            wcol = ((e - WORD_GROUPS[wgrp][0]) * PASSES + o) * 2 * H
             nc.tensor.matmul_mx(
                 out=up_bank(g, m)[:],
-                lhsT=xg[o][:, word_col(e) + j * TILE : word_col(e) + (j + 1) * TILE].bitcast(FP8X4),
+                lhsT=xg[o][:, word_col(g) : word_col(g) + TILE].bitcast(FP8X4),
                 lhsT_scale=token_scales(e, o, j),
                 rhs=(w1_sb, w3_sb)[m][wgrp][:, wcol : wcol + 2 * H].bitcast(FP4X4),
                 rhs_scale=(w1_pl, w3_pl)[m][grp][:, col : col + H],
@@ -222,12 +234,12 @@ def tile_moe_pkd_glu_silu_kernel(
 
         gather_bytes(0)
         gather_bytes(1)
-        for j in range(2):
-            gather_words(0, 0, j * TILE, (j + 1) * TILE)
-        gather_words(0, 1, 0, C)
-        for e in range(1, 3):
+        gather_words(0, 0, 1)
+        gather_words(0, 1, 2)
+        gather_words(1, 0, 2)
+        for g0, g1 in ((2, 4), (4, AHEAD)):
             for o in range(PASSES):
-                gather_words(e, o, 0, C)
+                gather_words(o, g0, g1)
         for o in range(PASSES):
             for g in range(2):
                 up_pass(g, 0, o)
@@ -243,8 +255,9 @@ def tile_moe_pkd_glu_silu_kernel(
                 for o in range(PASSES):
                     up_pass(g, m, o)
             gated(g)
-            if 3 <= e + 1 < E:
-                gather_words(e + 1, j, 0, C)
+            if AHEAD <= g + REUSE < TILES:
+                for o in range(PASSES):
+                    gather_words(o, g + REUSE, g + REUSE + 1)
             if j == 0 and e >= 2:
                 turn([g - 4, g - 3], up_bank(g, 0))
             if j == 0 and e >= 3:

@@ -25,8 +25,7 @@ TILE = 128
 TILES = S // TILE
 LIST = 16
 SCALE_GROUPS = ((0, 2), (2, 4), (4, 6))
-WORD_GROUPS = ((0, 1), (1, 2), (2, 3), (3, 4), (4, 6))
-BYTE_CHUNKS = ((0, 1), (1, 6))
+BYTE_CHUNKS = ((0, 1), (1, 3), (3, 6))
 AHEAD = 7
 REUSE = 3
 OUT_CHUNKS = ((0, 320), (320, 640), (640, 768))
@@ -56,15 +55,16 @@ def tile_moe_pkd_glu_silu_kernel(
         pos2_sb = held([P, T // LIST], U16, "pos2_sb")
         xs_win = held([P, T], U8, "xs_win")
         xw_win = held([P, PASSES * T], I32, "xw_win")
-        w1_sb = [held([P, (hi - lo) * PASSES * 2 * H], U8, f"w1_sb{lo}") for lo, hi in WORD_GROUPS]
-        w3_sb = [held([P, (hi - lo) * PASSES * 2 * H], U8, f"w3_sb{lo}") for lo, hi in WORD_GROUPS]
+        w1_sb = [held([P, PASSES * 2 * H], U8, f"w1_sb{e}") for e in range(E)]
+        w3_sb = [held([P, PASSES * 2 * H], U8, f"w3_sb{e}") for e in range(E)]
         w2_sb = held([P, E * 2 * N], U8, "w2_sb")
         w1_pl = [held([P, (hi - lo) * PASSES * H], U8, f"w1_pl{lo}") for lo, hi in SCALE_GROUPS]
         w3_pl = [held([P, (hi - lo) * PASSES * H], U8, f"w3_pl{lo}") for lo, hi in SCALE_GROUPS]
         w2_pl = held([P, E * N], U8, "w2_pl")
         gate_sb = held([P, 2 * T], F32, "gate_sb")
         xg = [held([P, AHEAD * TILE], U32, f"xg{o}") for o in range(PASSES)]
-        xs_both = [held([P, (hi - lo) * C], U8, f"xs_both{lo}") for lo, hi in BYTE_CHUNKS]
+        xs_outer = held([P, 3 * C], U8, "xs_outer")
+        xs_inner = held([P, 2 * C], U8, "xs_inner")
         xs_second = [held([P, (hi - lo) * C], U8, f"xs_second{lo}") for lo, hi in BYTE_CHUNKS]
         y_sb = held([P, S], F32, "y_sb")
         ident = held([P, P], F32, "ident")
@@ -86,11 +86,10 @@ def tile_moe_pkd_glu_silu_kernel(
         def load_scales(queue, m, grp):
             load_plane(queue, (w1_pl, w3_pl)[m][grp], (w1_scales, w3_scales)[m], *SCALE_GROUPS[grp])
 
-        def load_words(queue, m, grp):
-            lo, hi = WORD_GROUPS[grp]
-            queue.dma_start(
-                out=(w1_sb, w3_sb)[m][grp][:].bitcast(I32).rearrange("p (s b) -> p s b", s=(hi - lo) * PASSES),
-                in_=(w1_words, w3_words)[m][lo:hi].rearrange("e s p b -> p (e s) b").bitcast(I32),
+        def load_words(m, e):
+            nc.sync.dma_start(
+                out=(w1_sb, w3_sb)[m][e][:].bitcast(I32).rearrange("p (s b) -> p s b", s=PASSES),
+                in_=(w1_words, w3_words)[m][e].rearrange("s p b -> p s b").bitcast(I32),
             )
 
         zero(nc.gpsimd, xs_win[:])
@@ -101,6 +100,7 @@ def tile_moe_pkd_glu_silu_kernel(
         zero(nc.vector, w3_pl[0][:])
         zero(nc.gpsimd, xs_second[0][:])
         zero(nc.gpsimd, w3_pl[1][:])
+        zero(nc.gpsimd, xs_second[2][:])
         zero(nc.gpsimd, w2_pl[:])
         zero(nc.gpsimd, w3_pl[2][:])
         make_identity(nc, ident[:])
@@ -108,46 +108,40 @@ def tile_moe_pkd_glu_silu_kernel(
         nc.sync.dma_start(offs_sb[:], offs)
         token_rows = x_scales.rearrange("o (q r) t -> r q o t", r=4)
         for r in range(4):
-            nc.sync.dma_start(out=xs_win[r:P:16, :].bitcast(I32), in_=token_rows[r].bitcast(I32))
+            (nc.sync, nc.scalar)[r // 2].dma_start(out=xs_win[r:P:16, :].bitcast(I32), in_=token_rows[r].bitcast(I32))
         nc.sync.dma_start(
             out=xw_win[:].rearrange("p (o t) -> p o t", o=PASSES),
             in_=x_words.rearrange("o p t r -> p o (t r)").bitcast(I32),
         )
-        load_words(nc.sync, 0, 0)
-        load_words(nc.sync, 1, 0)
-        load_words(nc.sync, 1, 1)
-        load_words(nc.sync, 0, 1)
+        load_words(0, 0)
+        load_words(1, 0)
+        load_words(1, 1)
+        load_words(0, 1)
         load_scales(nc.scalar, 0, 0)
         load_scales(nc.scalar, 1, 0)
         for m in range(2):
             load_scales(nc.sync, m, 1)
         for grp in (2, 3):
-            load_words(nc.sync, 1, grp)
-            load_words(nc.sync, 0, grp)
-        load_plane(nc.sync, w2_pl, w2_scales, 0, E)
-        nc.sync.dma_start(
-            out=w2_sb[:].bitcast(I32).rearrange("p (e b) -> p e b", e=E),
-            in_=w2_words.rearrange("e s p b -> p (e s) b").bitcast(I32),
-        )
-        for m in range(2):
-            load_scales(nc.sync, m, 2)
-        load_words(nc.sync, 1, 4)
-        load_words(nc.sync, 0, 4)
-        nc.sync.dma_start(pos1_sb[:], pos1)
-        nc.sync.dma_start(pos2_sb[:], pos2)
-        nc.sync.dma_start(out=gate_sb[:].rearrange("n (r t) -> n r t", r=2), in_=gate.rearrange("r n t -> n r t"))
+            load_words(1, grp)
+            load_words(0, grp)
 
         def slots(lo, hi):
             return offs_sb[:, lo // LIST : hi // LIST]
 
-        def gather_bytes(c):
-            lo, hi = BYTE_CHUNKS[c]
-            for e0 in range(lo, hi, 2):
-                e1 = min(e0 + 2, hi)
-                nc.vector.tensor_copy(
-                    xs_both[c][:, (e0 - lo) * C : (e1 - lo) * C], xs_win[:].indirect(slots(e0 * C, e1 * C))
-                )
-            nc.scalar.dma_start(out=xs_second[c][0:112, :].bitcast(I32), in_=xs_both[c][16:P, :].bitcast(I32))
+        def byte_place(g):
+            if g < 2:
+                return xs_outer, C + g * TILE, 0, g * TILE
+            if g < 6:
+                return xs_inner, (g - 2) * TILE, 1, (g - 2) * TILE
+            col = (g - 3) * TILE if g < 9 else (g - 9) * TILE
+            return xs_outer, col, 2, col
+
+        def gather_bytes(g0, g1):
+            tile, col = byte_place(g0)[:2]
+            nc.vector.tensor_copy(tile[:, col : col + (g1 - g0) * TILE], xs_win[:].indirect(slots(g0 * TILE, g1 * TILE)))
+
+        def move_bytes(queue, c, src):
+            queue.dma_start(out=xs_second[c][0:112, :].bitcast(I32), in_=src[16:P, :].bitcast(I32))
 
         def word_col(g):
             return (g if g < AHEAD else AHEAD - REUSE + (g - AHEAD) % REUSE) * TILE
@@ -160,21 +154,20 @@ def tile_moe_pkd_glu_silu_kernel(
             )
 
         def token_scales(e, o, j):
-            c = group_of(BYTE_CHUNKS, e)
-            col = (e - BYTE_CHUNKS[c][0]) * C + j * TILE
-            return (xs_both, xs_second)[o][c][:, col : col + TILE]
+            tile, col, c, second_col = byte_place(2 * e + j)
+            if o == 0:
+                return tile[:, col : col + TILE]
+            return xs_second[c][:, second_col : second_col + TILE]
 
         def up_pass(g, m, o):
             e, j = divmod(g, 2)
             grp = group_of(SCALE_GROUPS, e)
             col = ((e - SCALE_GROUPS[grp][0]) * PASSES + o) * H
-            wgrp = group_of(WORD_GROUPS, e)
-            wcol = ((e - WORD_GROUPS[wgrp][0]) * PASSES + o) * 2 * H
             nc.tensor.matmul_mx(
                 out=up_bank(g, m)[:],
                 lhsT=xg[o][:, word_col(g) : word_col(g) + TILE].bitcast(FP8X4),
                 lhsT_scale=token_scales(e, o, j),
-                rhs=(w1_sb, w3_sb)[m][wgrp][:, wcol : wcol + 2 * H].bitcast(FP4X4),
+                rhs=(w1_sb, w3_sb)[m][e][:, o * 2 * H : (o + 1) * 2 * H].bitcast(FP4X4),
                 rhs_scale=(w1_pl, w3_pl)[m][grp][:, col : col + H],
                 start=(o == 0),
                 stop=(o == PASSES - 1),
@@ -232,8 +225,10 @@ def tile_moe_pkd_glu_silu_kernel(
             )
             nc.scalar.copy(y_sb[:, g * TILE : g * TILE + width], bank[:, :width])
 
-        gather_bytes(0)
-        gather_bytes(1)
+        gather_bytes(0, 2)
+        move_bytes(nc.scalar, 0, xs_outer[:, C : 2 * C])
+        gather_bytes(2, 6)
+        move_bytes(nc.scalar, 1, xs_inner[:])
         gather_words(0, 0, 1)
         gather_words(0, 1, 2)
         gather_words(1, 0, 2)
@@ -246,6 +241,23 @@ def tile_moe_pkd_glu_silu_kernel(
         for o in range(PASSES):
             for g in range(2):
                 up_pass(g, 1, o)
+        gather_bytes(6, 9)
+        gather_bytes(9, 12)
+        move_bytes(nc.sync, 2, xs_outer[:])
+        load_plane(nc.sync, w2_pl, w2_scales, 0, E)
+        nc.sync.dma_start(
+            out=w2_sb[:].bitcast(I32).rearrange("p (e b) -> p e b", e=E),
+            in_=w2_words.rearrange("e s p b -> p (e s) b").bitcast(I32),
+        )
+        for m in range(2):
+            load_scales(nc.sync, m, 2)
+        for e in (4, 5):
+            load_words(1, e)
+            load_words(0, e)
+        nc.sync.dma_start(pos1_sb[:], pos1)
+        nc.sync.dma_start(pos2_sb[:], pos2)
+        nc.sync.dma_start(out=gate_sb[:].rearrange("n (r t) -> n r t", r=2), in_=gate.rearrange("r n t -> n r t"))
+
         gated(0)
         gated(1)
 

@@ -26,8 +26,8 @@ TILES = S // TILE
 LIST = 16
 SCALE_GROUPS = ((0, 2), (2, 4), (4, 6))
 BYTE_CHUNKS = ((0, 1), (1, 3), (3, 6))
-AHEAD = 7
-REUSE = 3
+AHEAD = 6
+SHARED = 4
 OUT_CHUNKS = ((0, 320), (320, 640), (640, 768))
 
 
@@ -74,10 +74,10 @@ def tile_moe_pkd_glu_silu_kernel(
         def up_bank(g, m):
             return banks[2 * (g % 4) + m]
 
-        def load_plane(queue, plane, scales, lo, hi):
+        def load_plane(queue, plane, scales, lo, hi, live=range(4)):
             width = scales.shape[3]
             rows = scales[lo:hi].rearrange("e s (q r) i -> r q (e s) i", r=4)
-            for r in range(4):
+            for r in live:
                 queue.dma_start(
                     out=plane[r:P:32, :].bitcast(I32).rearrange("q (g i) -> q g i", i=width // 4),
                     in_=rows[r].bitcast(I32),
@@ -93,37 +93,20 @@ def tile_moe_pkd_glu_silu_kernel(
             )
 
         zero(nc.gpsimd, xs_win[:])
-        zero(nc.vector, xs_second[1][:])
-        zero(nc.vector, w1_pl[1][:])
-        zero(nc.vector, w1_pl[2][:])
-        zero(nc.vector, w1_pl[0][:])
         zero(nc.vector, w3_pl[0][:])
-        zero(nc.gpsimd, xs_second[0][:])
-        zero(nc.gpsimd, w3_pl[1][:])
-        zero(nc.gpsimd, xs_second[2][:])
-        zero(nc.gpsimd, w2_pl[:])
-        zero(nc.gpsimd, w3_pl[2][:])
-        make_identity(nc, ident[:])
+        zero(nc.vector, w1_pl[0][:])
+        zero(nc.vector, xs_second[0][:])
+        zero(nc.vector, xs_second[1][:])
+        zero(nc.gpsimd, w1_pl[1][:])
 
         nc.sync.dma_start(offs_sb[:], offs)
         token_rows = x_scales.rearrange("o (q r) t -> r q o t", r=4)
         for r in range(4):
-            (nc.sync, nc.scalar)[r // 2].dma_start(out=xs_win[r:P:16, :].bitcast(I32), in_=token_rows[r].bitcast(I32))
+            (nc.scalar, nc.sync)[r // 2].dma_start(out=xs_win[r:P:16, :].bitcast(I32), in_=token_rows[r].bitcast(I32))
         nc.sync.dma_start(
             out=xw_win[:].rearrange("p (o t) -> p o t", o=PASSES),
             in_=x_words.rearrange("o p t r -> p o (t r)").bitcast(I32),
         )
-        load_words(0, 0)
-        load_words(1, 0)
-        load_words(1, 1)
-        load_words(0, 1)
-        load_scales(nc.scalar, 0, 0)
-        load_scales(nc.scalar, 1, 0)
-        for m in range(2):
-            load_scales(nc.sync, m, 1)
-        for grp in (2, 3):
-            load_words(1, grp)
-            load_words(0, grp)
 
         def slots(lo, hi):
             return offs_sb[:, lo // LIST : hi // LIST]
@@ -144,7 +127,7 @@ def tile_moe_pkd_glu_silu_kernel(
             queue.dma_start(out=xs_second[c][0:112, :].bitcast(I32), in_=src[16:P, :].bitcast(I32))
 
         def word_col(g):
-            return (g if g < AHEAD else AHEAD - REUSE + (g - AHEAD) % REUSE) * TILE
+            return (g % AHEAD) * TILE
 
         def gather_words(o, g0, g1):
             window = xw_win[:, o * T : (o + 1) * T].bitcast(U32)
@@ -184,12 +167,17 @@ def tile_moe_pkd_glu_silu_kernel(
                 act[:].rearrange("s (u p d) -> s u p d", u=2, d=2), by_word_half(up_bank(g, 0)), SILU
             )
             h = held([P, H], BF16, f"h{g}")
-            nc.vector.tensor_tensor(
-                h[:].rearrange("s (u p d) -> s u p d", u=2, d=2),
-                by_word_half(up_bank(g, 1)),
-                act[:].rearrange("s (u p d) -> s u p d", u=2, d=2),
-                MULT,
-            )
+            if g < SHARED:
+                lin = ring.tile([P, H], F32, name="lin", bufs=4, align_bytes=64)
+                nc.scalar.copy(lin[:].rearrange("s (u p d) -> s u p d", u=2, d=2), by_word_half(up_bank(g, 1)))
+                nc.gpsimd.tensor_tensor(h[:], lin[:], act[:], MULT)
+            else:
+                nc.vector.tensor_tensor(
+                    h[:].rearrange("s (u p d) -> s u p d", u=2, d=2),
+                    by_word_half(up_bank(g, 1)),
+                    act[:].rearrange("s (u p d) -> s u p d", u=2, d=2),
+                    MULT,
+                )
             h_tiles[g] = h
 
         packed = {}
@@ -211,28 +199,50 @@ def tile_moe_pkd_glu_silu_kernel(
             nc.vector.quantize_mx(out=codes[:].bitcast(FP8X4), scales=h_scales[:], in_=h_turned[:])
             packed[tiles[0]] = (codes, h_scales, width)
 
-        def down(g, bank):
-            codes, h_scales, width = packed[g]
-            e = g // 2
-            nc.tensor.matmul_mx(
-                out=bank[:, :width],
-                lhsT=w2_sb[:, e * 2 * N : (e + 1) * 2 * N].bitcast(FP4X4),
-                lhsT_scale=w2_pl[:, e * N : (e + 1) * N],
-                rhs=codes[:].bitcast(FP8X4),
-                rhs_scale=h_scales[:],
-                start=True,
-                stop=True,
-            )
-            nc.scalar.copy(y_sb[:, g * TILE : g * TILE + width], bank[:, :width])
+        def down(firsts, bank):
+            col = 0
+            for g in firsts:
+                codes, h_scales, width = packed[g]
+                e = g // 2
+                nc.tensor.matmul_mx(
+                    out=bank[:, col : col + width],
+                    lhsT=w2_sb[:, e * 2 * N : (e + 1) * 2 * N].bitcast(FP4X4),
+                    lhsT_scale=w2_pl[:, e * N : (e + 1) * N],
+                    rhs=codes[:].bitcast(FP8X4),
+                    rhs_scale=h_scales[:],
+                    start=True,
+                    stop=True,
+                )
+                col = col + width
+            nc.scalar.copy(y_sb[:, firsts[0] * TILE : firsts[0] * TILE + col], bank[:, :col])
 
         gather_bytes(0, 2)
-        move_bytes(nc.scalar, 0, xs_outer[:, C : 2 * C])
         gather_bytes(2, 6)
-        move_bytes(nc.scalar, 1, xs_inner[:])
+        load_words(0, 0)
+        load_scales(nc.sync, 0, 0)
+        move_bytes(nc.sync, 0, xs_outer[:, C : 2 * C])
+        load_words(1, 0)
+        load_plane(nc.sync, w3_pl[0], w3_scales, *SCALE_GROUPS[0], range(1))
+        move_bytes(nc.sync, 1, xs_inner[:])
+        load_plane(nc.gpsimd, w3_pl[0], w3_scales, *SCALE_GROUPS[0], range(1, 4))
+        zero(nc.gpsimd, w3_pl[1][:])
+        zero(nc.gpsimd, w1_pl[2][:])
+        zero(nc.gpsimd, w3_pl[2][:])
+        zero(nc.gpsimd, xs_second[2][:])
+        zero(nc.gpsimd, w2_pl[:])
+        make_identity(nc, ident[:])
+        load_words(1, 1)
+        load_words(0, 1)
+        for m in range(2):
+            load_scales(nc.sync, m, 1)
+        for grp in (2, 3):
+            load_words(1, grp)
+            load_words(0, grp)
+
         gather_words(0, 0, 1)
         gather_words(0, 1, 2)
         gather_words(1, 0, 2)
-        for g0, g1 in ((2, 4), (4, AHEAD)):
+        for g0, g1 in ((2, 4), (4, 6)):
             for o in range(PASSES):
                 gather_words(o, g0, g1)
         for o in range(PASSES):
@@ -258,31 +268,38 @@ def tile_moe_pkd_glu_silu_kernel(
         nc.sync.dma_start(pos2_sb[:], pos2)
         nc.sync.dma_start(out=gate_sb[:].rearrange("n (r t) -> n r t", r=2), in_=gate.rearrange("r n t -> n r t"))
 
+        for o in range(PASSES):
+            gather_words(o, 6, 8)
         gated(0)
         gated(1)
 
         for g in range(2, TILES):
-            e, j = divmod(g, 2)
             for m in range(2):
                 for o in range(PASSES):
                     up_pass(g, m, o)
             gated(g)
-            if AHEAD <= g + REUSE < TILES:
+            if g in (3, 5):
                 for o in range(PASSES):
-                    gather_words(o, g + REUSE, g + REUSE + 1)
-            if j == 0 and e >= 2:
-                turn([g - 4, g - 3], up_bank(g, 0))
-            if j == 0 and e >= 3:
-                down(g - 6, up_bank(g, 1))
+                    gather_words(o, g + 5, g + 7)
+            if g == 4:
+                turn([0, 1], up_bank(g, 0))
+            if g == 6:
+                turn([2, 3], up_bank(g, 0))
+                down([0], up_bank(g, 1))
+            if g == 8:
+                turn([4, 5], up_bank(g, 0))
+                turn([6, 7], up_bank(g, 1))
+            if g == 9:
+                down([2], up_bank(g, 0))
+            if g == 10:
+                turn([8, 9], up_bank(g, 0))
+                down([4, 6], up_bank(g, 1))
 
-        last = TILES - 1
-        turn([last - 3, last - 2], up_bank(last, 0))
-        down(last - 5, up_bank(last - 2, 1))
-        turn([last - 1], up_bank(last - 2, 0))
-        down(last - 3, up_bank(last - 3, 1))
-        turn([last], up_bank(last - 3, 0))
-        down(last - 1, up_bank(last - 1, 1))
-        down(last, up_bank(last, 1))
+        turn([10], up_bank(9, 0))
+        down([8], up_bank(9, 1))
+        turn([11], up_bank(8, 0))
+        down([10], up_bank(8, 1))
+        down([11], up_bank(11, 0))
 
         def weighted(r, lo, hi):
             part = ring.tile([P, 320], F32, name=f"part{r}")

@@ -25,10 +25,10 @@ TILE = 128
 TILES = S // TILE
 LIST = 16
 SCALE_GROUPS = ((0, 2), (2, 4), (4, 6))
-BYTE_CHUNKS = ((0, 1), (1, 3), (3, 6))
-AHEAD = 6
+BYTE_COLS = (3 * TILE, 0, 6 * TILE)
+WORD_TILES = (0, 1, 4, 5, 0, 1, 2, 3, 4, 5, 6, 7)
 SHARED = 4
-OUT_CHUNKS = ((0, 320), (320, 640), (640, 768))
+OUT_CHUNKS = ((0, 384), (384, 640), (640, 768))
 
 
 def group_of(groups, e):
@@ -54,7 +54,7 @@ def tile_moe_pkd_glu_silu_kernel(
         pos1_sb = held([P, T // LIST], U16, "pos1_sb")
         pos2_sb = held([P, T // LIST], U16, "pos2_sb")
         xs_win = held([P, T], U8, "xs_win")
-        xw_win = held([P, PASSES * T], I32, "xw_win")
+        xw_win = [held([P, T], I32, f"xw_win{o}") for o in range(PASSES)]
         w1_sb = [held([P, PASSES * 2 * H], U8, f"w1_sb{e}") for e in range(E)]
         w3_sb = [held([P, PASSES * 2 * H], U8, f"w3_sb{e}") for e in range(E)]
         w2_sb = held([P, E * 2 * N], U8, "w2_sb")
@@ -62,10 +62,9 @@ def tile_moe_pkd_glu_silu_kernel(
         w3_pl = [held([P, (hi - lo) * PASSES * H], U8, f"w3_pl{lo}") for lo, hi in SCALE_GROUPS]
         w2_pl = held([P, E * N], U8, "w2_pl")
         gate_sb = held([P, 2 * T], F32, "gate_sb")
-        xg = [held([P, AHEAD * TILE], U32, f"xg{o}") for o in range(PASSES)]
-        xs_outer = held([P, 3 * C], U8, "xs_outer")
-        xs_inner = held([P, 2 * C], U8, "xs_inner")
-        xs_second = [held([P, (hi - lo) * C], U8, f"xs_second{lo}") for lo, hi in BYTE_CHUNKS]
+        xg = [held([P, 8 * TILE], U32, f"xg{o}") for o in range(PASSES)]
+        xs_first = held([P, 10 * TILE], U8, "xs_first")
+        xs_second = [held([P, 4 * TILE], U8, f"xs_second{c}") for c in range(3)]
         y_sb = held([P, S], F32, "y_sb")
         ident = held([P, P], F32, "ident")
 
@@ -92,55 +91,47 @@ def tile_moe_pkd_glu_silu_kernel(
                 in_=(w1_words, w3_words)[m][e].rearrange("s p b -> p s b").bitcast(I32),
             )
 
-        zero(nc.gpsimd, xs_win[:])
-        zero(nc.vector, w3_pl[0][:])
+        zero(nc.vector, xs_win[:])
+        zero(nc.gpsimd, w3_pl[0][:])
         zero(nc.vector, w1_pl[0][:])
         zero(nc.vector, xs_second[0][:])
         zero(nc.vector, xs_second[1][:])
-        zero(nc.gpsimd, w1_pl[1][:])
+        zero(nc.vector, w1_pl[1][:])
+        zero(nc.vector, w3_pl[1][:])
 
         nc.sync.dma_start(offs_sb[:], offs)
         token_rows = x_scales.rearrange("o (q r) t -> r q o t", r=4)
         for r in range(4):
             (nc.scalar, nc.sync)[r // 2].dma_start(out=xs_win[r:P:16, :].bitcast(I32), in_=token_rows[r].bitcast(I32))
-        nc.sync.dma_start(
-            out=xw_win[:].rearrange("p (o t) -> p o t", o=PASSES),
-            in_=x_words.rearrange("o p t r -> p o (t r)").bitcast(I32),
-        )
 
         def slots(lo, hi):
             return offs_sb[:, lo // LIST : hi // LIST]
 
-        def byte_place(g):
-            if g < 2:
-                return xs_outer, C + g * TILE, 0, g * TILE
-            if g < 6:
-                return xs_inner, (g - 2) * TILE, 1, (g - 2) * TILE
-            col = (g - 3) * TILE if g < 9 else (g - 9) * TILE
-            return xs_outer, col, 2, col
+        def byte_cols(c):
+            return xs_first[:, BYTE_COLS[c] : BYTE_COLS[c] + 4 * TILE]
 
-        def gather_bytes(g0, g1):
-            tile, col = byte_place(g0)[:2]
-            nc.vector.tensor_copy(tile[:, col : col + (g1 - g0) * TILE], xs_win[:].indirect(slots(g0 * TILE, g1 * TILE)))
+        def gather_bytes(c):
+            nc.vector.tensor_copy(byte_cols(c), xs_win[:].indirect(slots(c * 4 * TILE, (c + 1) * 4 * TILE)))
 
-        def move_bytes(queue, c, src):
-            queue.dma_start(out=xs_second[c][0:112, :].bitcast(I32), in_=src[16:P, :].bitcast(I32))
+        def move_bytes(c):
+            nc.sync.dma_start(out=xs_second[c][0:112, :].bitcast(I32), in_=byte_cols(c)[16:P, :].bitcast(I32))
+
+        def load_tokens(o):
+            nc.sync.dma_start(out=xw_win[o][:], in_=x_words[o].rearrange("p t r -> p (t r)").bitcast(I32))
 
         def word_col(g):
-            return (g % AHEAD) * TILE
+            return WORD_TILES[g] * TILE
 
         def gather_words(o, g0, g1):
-            window = xw_win[:, o * T : (o + 1) * T].bitcast(U32)
+            window = xw_win[o][:].bitcast(U32)
             col = word_col(g0)
             nc.vector.tensor_copy(
                 xg[o][:, col : col + (g1 - g0) * TILE], window.indirect(slots(g0 * TILE, g1 * TILE))
             )
 
         def token_scales(e, o, j):
-            tile, col, c, second_col = byte_place(2 * e + j)
-            if o == 0:
-                return tile[:, col : col + TILE]
-            return xs_second[c][:, second_col : second_col + TILE]
+            c, place = divmod(2 * e + j, 4)
+            return (byte_cols(c), xs_second[c])[o][:, place * TILE : (place + 1) * TILE]
 
         def up_pass(g, m, o):
             e, j = divmod(g, 2)
@@ -199,7 +190,7 @@ def tile_moe_pkd_glu_silu_kernel(
             nc.vector.quantize_mx(out=codes[:].bitcast(FP8X4), scales=h_scales[:], in_=h_turned[:])
             packed[tiles[0]] = (codes, h_scales, width)
 
-        def down(firsts, bank):
+        def down(firsts, bank, copy_out):
             col = 0
             for g in firsts:
                 codes, h_scales, width = packed[g]
@@ -214,46 +205,47 @@ def tile_moe_pkd_glu_silu_kernel(
                     stop=True,
                 )
                 col = col + width
-            nc.scalar.copy(y_sb[:, firsts[0] * TILE : firsts[0] * TILE + col], bank[:, :col])
+            copy_out(y_sb[:, firsts[0] * TILE : firsts[0] * TILE + col], bank[:, :col])
 
-        gather_bytes(0, 2)
-        gather_bytes(2, 6)
+        gather_bytes(0)
+        load_tokens(0)
         load_words(0, 0)
         load_scales(nc.sync, 0, 0)
-        move_bytes(nc.sync, 0, xs_outer[:, C : 2 * C])
         load_words(1, 0)
         load_plane(nc.sync, w3_pl[0], w3_scales, *SCALE_GROUPS[0], range(1))
-        move_bytes(nc.sync, 1, xs_inner[:])
-        load_plane(nc.gpsimd, w3_pl[0], w3_scales, *SCALE_GROUPS[0], range(1, 4))
-        zero(nc.gpsimd, w3_pl[1][:])
+        load_tokens(1)
+        load_plane(nc.sync, w3_pl[0], w3_scales, *SCALE_GROUPS[0], range(1, 2))
+        move_bytes(0)
+        load_plane(nc.gpsimd, w3_pl[0], w3_scales, *SCALE_GROUPS[0], range(2, 4))
+        zero(nc.gpsimd, xs_second[2][:])
         zero(nc.gpsimd, w1_pl[2][:])
         zero(nc.gpsimd, w3_pl[2][:])
-        zero(nc.gpsimd, xs_second[2][:])
         zero(nc.gpsimd, w2_pl[:])
         make_identity(nc, ident[:])
         load_words(1, 1)
         load_words(0, 1)
         for m in range(2):
             load_scales(nc.sync, m, 1)
-        for grp in (2, 3):
-            load_words(1, grp)
-            load_words(0, grp)
+        load_words(1, 2)
+        load_words(0, 2)
 
         gather_words(0, 0, 1)
         gather_words(0, 1, 2)
         gather_words(1, 0, 2)
-        for g0, g1 in ((2, 4), (4, 6)):
-            for o in range(PASSES):
-                gather_words(o, g0, g1)
         for o in range(PASSES):
+            gather_words(o, 2, 4)
+        for m in range(2):
             for g in range(2):
-                up_pass(g, 0, o)
-        for o in range(PASSES):
-            for g in range(2):
-                up_pass(g, 1, o)
-        gather_bytes(6, 9)
-        gather_bytes(9, 12)
-        move_bytes(nc.sync, 2, xs_outer[:])
+                up_pass(g, m, 0)
+        gather_bytes(1)
+        move_bytes(1)
+        gather_words(0, 4, 8)
+        for g in range(2):
+            for m in range(2):
+                up_pass(g, m, 1)
+        gather_words(1, 4, 8)
+        load_words(1, 3)
+        load_words(0, 3)
         load_plane(nc.sync, w2_pl, w2_scales, 0, E)
         nc.sync.dma_start(
             out=w2_sb[:].bitcast(I32).rearrange("p (e b) -> p e b", e=E),
@@ -261,15 +253,9 @@ def tile_moe_pkd_glu_silu_kernel(
         )
         for m in range(2):
             load_scales(nc.sync, m, 2)
-        for e in (4, 5):
-            load_words(1, e)
-            load_words(0, e)
-        nc.sync.dma_start(pos1_sb[:], pos1)
-        nc.sync.dma_start(pos2_sb[:], pos2)
-        nc.sync.dma_start(out=gate_sb[:].rearrange("n (r t) -> n r t", r=2), in_=gate.rearrange("r n t -> n r t"))
+        load_words(1, 4)
+        load_words(0, 4)
 
-        for o in range(PASSES):
-            gather_words(o, 6, 8)
         gated(0)
         gated(1)
 
@@ -277,46 +263,54 @@ def tile_moe_pkd_glu_silu_kernel(
             for m in range(2):
                 for o in range(PASSES):
                     up_pass(g, m, o)
-            gated(g)
-            if g in (3, 5):
+            if g == 3:
+                gather_bytes(2)
                 for o in range(PASSES):
-                    gather_words(o, g + 5, g + 7)
+                    gather_words(o, 8, 12)
+                move_bytes(2)
+                load_words(1, 5)
+                load_words(0, 5)
+                nc.sync.dma_start(pos1_sb[:], pos1)
+                nc.sync.dma_start(pos2_sb[:], pos2)
+                nc.sync.dma_start(
+                    out=gate_sb[:].rearrange("n (r t) -> n r t", r=2), in_=gate.rearrange("r n t -> n r t")
+                )
+            gated(g)
             if g == 4:
                 turn([0, 1], up_bank(g, 0))
             if g == 6:
                 turn([2, 3], up_bank(g, 0))
-                down([0], up_bank(g, 1))
+                down([0], up_bank(g, 1), nc.scalar.copy)
             if g == 8:
                 turn([4, 5], up_bank(g, 0))
                 turn([6, 7], up_bank(g, 1))
             if g == 9:
-                down([2], up_bank(g, 0))
-            if g == 10:
-                turn([8, 9], up_bank(g, 0))
-                down([4, 6], up_bank(g, 1))
+                down([2], up_bank(g, 0), nc.scalar.copy)
 
+        turn([8, 9], up_bank(10, 0))
+        down([4, 6], up_bank(10, 1), nc.vector.tensor_copy)
         turn([10], up_bank(9, 0))
-        down([8], up_bank(9, 1))
+        down([8], up_bank(9, 1), nc.scalar.copy)
         turn([11], up_bank(8, 0))
-        down([10], up_bank(8, 1))
-        down([11], up_bank(11, 0))
+        down([10], up_bank(8, 1), nc.scalar.copy)
+        down([11], up_bank(11, 0), nc.scalar.copy)
+
+        parts = [held([P, T], F32, f"part{r}") for r in range(2)]
 
         def weighted(r, lo, hi):
-            part = ring.tile([P, 320], F32, name=f"part{r}")
             pos_sb = (pos1_sb, pos2_sb)[r]
             nc.vector.tensor_tensor(
-                part[:, : hi - lo],
+                parts[r][:, lo:hi],
                 y_sb[:].indirect(pos_sb[:, lo // LIST : hi // LIST]),
                 gate_sb[:, r * T + lo : r * T + hi],
                 MULT,
             )
-            return part
 
-        first = weighted(0, *OUT_CHUNKS[0])
+        weighted(0, 0, T)
+        weighted(1, *OUT_CHUNKS[0])
         for c, (lo, hi) in enumerate(OUT_CHUNKS):
-            second = weighted(1, lo, hi)
-            ahead = weighted(0, *OUT_CHUNKS[c + 1]) if c + 1 < len(OUT_CHUNKS) else None
-            total = ring.tile([P, 320], F32, name="total")
-            nc.vector.tensor_tensor(total[:, : hi - lo], first[:, : hi - lo], second[:, : hi - lo], ADD)
-            nc.sync.dma_start(out=out[:, lo:hi], in_=total[:, : hi - lo])
-            first = ahead
+            if c + 1 < len(OUT_CHUNKS):
+                weighted(1, *OUT_CHUNKS[c + 1])
+            total = held([P, hi - lo], F32, f"total{c}")
+            nc.vector.tensor_tensor(total[:], parts[0][:, lo:hi], parts[1][:, lo:hi], ADD)
+            nc.sync.dma_start(out=out[:, lo:hi], in_=total[:])

@@ -24,9 +24,9 @@ PASSES = 2
 TILE = 128
 TILES = S // TILE
 LIST = 16
-SCALE_GROUPS = ((0, 2), (2, 4), (4, 6))
+SCALE_GROUPS = ((0, 3), (3, 6))
 BYTE_COLS = (3 * TILE, 0, 6 * TILE)
-WORD_TILES = (0, 1, 4, 5, 0, 1, 2, 3, 4, 5, 6, 7)
+WORD_TILES = (0, 1, 4, 5, 0, 1, 2, 3, 4, 5, 2, 3)
 SHARED = 4
 OUT_CHUNKS = ((0, 384), (384, 640), (640, 768))
 
@@ -41,11 +41,10 @@ def tile_moe_pkd_glu_silu_kernel(
     nc = tc.nc
     with ExitStack() as ctx:
         keep = ctx.enter_context(tc.tile_pool(name="keep", bufs=1))
-        ring = ctx.enter_context(tc.tile_pool(name="ring", bufs=3))
         psum = ctx.enter_context(tc.psum_pool(name="psum", bufs=1))
 
         def held(shape, dtype, name):
-            return keep.tile(shape, dtype, name=name, align_bytes=64)
+            return keep.tile(shape, dtype, name=name, align_bytes=256)
 
         def zero(engine, tile_ap):
             engine.memset(tile_ap.bitcast(I32), 0)
@@ -62,7 +61,7 @@ def tile_moe_pkd_glu_silu_kernel(
         w3_pl = [held([P, (hi - lo) * PASSES * H], U8, f"w3_pl{lo}") for lo, hi in SCALE_GROUPS]
         w2_pl = held([P, E * N], U8, "w2_pl")
         gate_sb = held([P, 2 * T], F32, "gate_sb")
-        xg = [held([P, 8 * TILE], U32, f"xg{o}") for o in range(PASSES)]
+        xg = [held([P, 6 * TILE], U32, f"xg{o}") for o in range(PASSES)]
         xs_first = held([P, 10 * TILE], U8, "xs_first")
         xs_second = [held([P, 4 * TILE], U8, f"xs_second{c}") for c in range(3)]
         y_sb = held([P, S], F32, "y_sb")
@@ -97,7 +96,6 @@ def tile_moe_pkd_glu_silu_kernel(
         zero(nc.vector, xs_second[0][:])
         zero(nc.vector, xs_second[1][:])
         zero(nc.vector, w1_pl[1][:])
-        zero(nc.vector, w3_pl[1][:])
 
         nc.sync.dma_start(offs_sb[:], offs)
         token_rows = x_scales.rearrange("o (q r) t -> r q o t", r=4)
@@ -153,13 +151,13 @@ def tile_moe_pkd_glu_silu_kernel(
         h_tiles = {}
 
         def gated(g):
-            act = ring.tile([P, H], F32, name="act", bufs=4, align_bytes=64)
+            act = held([P, H], F32, f"act{g}")
             nc.scalar.activation(
                 act[:].rearrange("s (u p d) -> s u p d", u=2, d=2), by_word_half(up_bank(g, 0)), SILU
             )
             h = held([P, H], BF16, f"h{g}")
             if g < SHARED:
-                lin = ring.tile([P, H], F32, name="lin", bufs=4, align_bytes=64)
+                lin = held([P, H], F32, f"lin{g}")
                 nc.scalar.copy(lin[:].rearrange("s (u p d) -> s u p d", u=2, d=2), by_word_half(up_bank(g, 1)))
                 nc.gpsimd.tensor_tensor(h[:], lin[:], act[:], MULT)
             else:
@@ -218,16 +216,15 @@ def tile_moe_pkd_glu_silu_kernel(
         move_bytes(0)
         load_plane(nc.gpsimd, w3_pl[0], w3_scales, *SCALE_GROUPS[0], range(2, 4))
         zero(nc.gpsimd, xs_second[2][:])
-        zero(nc.gpsimd, w1_pl[2][:])
-        zero(nc.gpsimd, w3_pl[2][:])
+        zero(nc.gpsimd, w3_pl[1][:])
         zero(nc.gpsimd, w2_pl[:])
         make_identity(nc, ident[:])
         load_words(1, 1)
         load_words(0, 1)
-        for m in range(2):
-            load_scales(nc.sync, m, 1)
         load_words(1, 2)
         load_words(0, 2)
+        for m in range(2):
+            load_scales(nc.sync, m, 1)
 
         gather_words(0, 0, 1)
         gather_words(0, 1, 2)
@@ -246,52 +243,55 @@ def tile_moe_pkd_glu_silu_kernel(
         gather_words(1, 4, 8)
         load_words(1, 3)
         load_words(0, 3)
-        load_plane(nc.sync, w2_pl, w2_scales, 0, E)
-        nc.sync.dma_start(
-            out=w2_sb[:].bitcast(I32).rearrange("p (e b) -> p e b", e=E),
-            in_=w2_words.rearrange("e s p b -> p (e s) b").bitcast(I32),
-        )
-        for m in range(2):
-            load_scales(nc.sync, m, 2)
         load_words(1, 4)
         load_words(0, 4)
 
         gated(0)
         gated(1)
 
-        for g in range(2, TILES):
+        for g in range(2, TILES - 2):
             for m in range(2):
                 for o in range(PASSES):
                     up_pass(g, m, o)
             if g == 3:
                 gather_bytes(2)
                 for o in range(PASSES):
-                    gather_words(o, 8, 12)
+                    gather_words(o, 8, 10)
                 move_bytes(2)
                 load_words(1, 5)
                 load_words(0, 5)
+                load_plane(nc.sync, w2_pl, w2_scales, 0, E)
+                nc.sync.dma_start(
+                    out=w2_sb[:].bitcast(I32).rearrange("p (e b) -> p e b", e=E),
+                    in_=w2_words.rearrange("e s p b -> p (e s) b").bitcast(I32),
+                )
                 nc.sync.dma_start(pos1_sb[:], pos1)
                 nc.sync.dma_start(pos2_sb[:], pos2)
                 nc.sync.dma_start(
                     out=gate_sb[:].rearrange("n (r t) -> n r t", r=2), in_=gate.rearrange("r n t -> n r t")
                 )
             gated(g)
-            if g == 4:
-                turn([0, 1], up_bank(g, 0))
-            if g == 6:
-                turn([2, 3], up_bank(g, 0))
-                down([0], up_bank(g, 1), nc.scalar.copy)
-            if g == 8:
-                turn([4, 5], up_bank(g, 0))
-                turn([6, 7], up_bank(g, 1))
+            if g == 7:
+                turn([0, 1], up_bank(6, 0))
+                turn([2, 3], up_bank(6, 1))
+                for o in range(PASSES):
+                    gather_words(o, 10, 12)
             if g == 9:
-                down([2], up_bank(g, 0), nc.scalar.copy)
+                turn([4, 5], up_bank(8, 0))
+                turn([6, 7], up_bank(8, 1))
 
+        for m in range(2):
+            for g in (10, 11):
+                for o in range(PASSES):
+                    up_pass(g, m, o)
+        gated(10)
+        gated(11)
         turn([8, 9], up_bank(10, 0))
-        down([4, 6], up_bank(10, 1), nc.vector.tensor_copy)
+        down([0, 2], up_bank(10, 1), nc.vector.tensor_copy)
         turn([10], up_bank(9, 0))
-        down([8], up_bank(9, 1), nc.scalar.copy)
         turn([11], up_bank(8, 0))
+        down([4, 6], up_bank(11, 1), nc.scalar.copy)
+        down([8], up_bank(9, 1), nc.scalar.copy)
         down([10], up_bank(8, 1), nc.scalar.copy)
         down([11], up_bank(11, 0), nc.scalar.copy)
 

@@ -24,7 +24,7 @@ PASSES = 2
 TILE = 128
 TILES = S // TILE
 LIST = 16
-SCALE_GROUPS = ((0, 3), (3, 6))
+SCALE_GROUPS = ((0, 2), (2, 6))
 BYTE_COLS = (3 * TILE, 0, 6 * TILE)
 WORD_TILES = (0, 1, 4, 5, 0, 1, 2, 3, 4, 5, 2, 3)
 SHARED = 4
@@ -90,7 +90,7 @@ def tile_moe_pkd_glu_silu_kernel(
                 in_=(w1_words, w3_words)[m][e].rearrange("s p b -> p s b").bitcast(I32),
             )
 
-        zero(nc.vector, xs_win[:])
+        zero(nc.gpsimd, xs_win[:])
         zero(nc.gpsimd, w3_pl[0][:])
         zero(nc.vector, w1_pl[0][:])
         zero(nc.vector, xs_second[0][:])
@@ -250,9 +250,15 @@ def tile_moe_pkd_glu_silu_kernel(
         gated(1)
 
         for g in range(2, TILES - 2):
-            for m in range(2):
+            if g == 4:
                 for o in range(PASSES):
-                    up_pass(g, m, o)
+                    for tile in (4, 5):
+                        for m in range(2):
+                            up_pass(tile, m, o)
+            elif g != 5:
+                for m in range(2):
+                    for o in range(PASSES):
+                        up_pass(g, m, o)
             if g == 3:
                 gather_bytes(2)
                 for o in range(PASSES):

@@ -24,7 +24,7 @@ PASSES = 2
 TILE = 128
 TILES = S // TILE
 LIST = 16
-SCALE_GROUPS = ((0, 2), (2, 6))
+SCALE_GROUPS = ((0, 2), (2, 4), (4, 6))
 BYTE_COLS = (3 * TILE, 0, 6 * TILE)
 WORD_TILES = (0, 1, 4, 5, 0, 1, 2, 3, 4, 5, 2, 3)
 SHARED = 4
@@ -217,14 +217,16 @@ def tile_moe_pkd_glu_silu_kernel(
         load_plane(nc.gpsimd, w3_pl[0], w3_scales, *SCALE_GROUPS[0], range(2, 4))
         zero(nc.gpsimd, xs_second[2][:])
         zero(nc.gpsimd, w3_pl[1][:])
+        zero(nc.gpsimd, w1_pl[2][:])
+        zero(nc.gpsimd, w3_pl[2][:])
         zero(nc.gpsimd, w2_pl[:])
         make_identity(nc, ident[:])
         load_words(1, 1)
         load_words(0, 1)
+        load_scales(nc.sync, 0, 1)
         load_words(1, 2)
         load_words(0, 2)
-        for m in range(2):
-            load_scales(nc.sync, m, 1)
+        load_scales(nc.sync, 1, 1)
 
         gather_words(0, 0, 1)
         gather_words(0, 1, 2)
@@ -243,19 +245,28 @@ def tile_moe_pkd_glu_silu_kernel(
         gather_words(1, 4, 8)
         load_words(1, 3)
         load_words(0, 3)
+        load_scales(nc.sync, 0, 2)
         load_words(1, 4)
         load_words(0, 4)
+        load_scales(nc.sync, 1, 2)
 
         gated(0)
         gated(1)
 
         for g in range(2, TILES - 2):
-            if g == 4:
-                for o in range(PASSES):
-                    for tile in (4, 5):
+            if g in (4, 8):
+                for m in range(2):
+                    for tile in (g, g + 1):
+                        up_pass(tile, m, 0)
+                if g == 4:
+                    for tile in (g, g + 1):
                         for m in range(2):
-                            up_pass(tile, m, o)
-            elif g != 5:
+                            up_pass(tile, m, 1)
+                else:
+                    for m in range(2):
+                        for tile in (g, g + 1):
+                            up_pass(tile, m, 1)
+            elif g not in (5, 9):
                 for m in range(2):
                     for o in range(PASSES):
                         up_pass(g, m, o)
@@ -278,13 +289,13 @@ def tile_moe_pkd_glu_silu_kernel(
                 )
             gated(g)
             if g == 7:
-                turn([0, 1], up_bank(6, 0))
-                turn([2, 3], up_bank(6, 1))
                 for o in range(PASSES):
                     gather_words(o, 10, 12)
             if g == 9:
-                turn([4, 5], up_bank(8, 0))
-                turn([6, 7], up_bank(8, 1))
+                turn([0, 1], up_bank(8, 0))
+                turn([2, 3], up_bank(9, 0))
+                turn([4, 5], up_bank(8, 1))
+                turn([6, 7], up_bank(9, 1))
 
         for m in range(2):
             for g in (10, 11):

@@ -25,8 +25,8 @@ TILE = 128
 TILES = S // TILE
 LIST = 16
 SCALE_GROUPS = ((0, 2), (2, 4), (4, 6))
-BYTE_COLS = (3 * TILE, 0, 6 * TILE)
-WORD_TILES = (0, 1, 4, 5, 0, 1, 2, 3, 4, 5, 2, 3)
+BYTE_COLS = (6 * TILE, 3 * TILE, 0)
+WORD_TILES = ((0, 1, 2, 3, 3, 4, 5, 6, 11, 12, 5, 6), (10, 11, 12, 13, 7, 8, 9, 10, 13, 14, 9, 10))
 SHARED = 4
 OUT_CHUNKS = ((0, 384), (384, 640), (640, 768))
 
@@ -54,14 +54,15 @@ def tile_moe_pkd_glu_silu_kernel(
         pos2_sb = held([P, T // LIST], U16, "pos2_sb")
         xs_win = held([P, T], U8, "xs_win")
         xw_win = [held([P, T], I32, f"xw_win{o}") for o in range(PASSES)]
-        w1_sb = [held([P, PASSES * 2 * H], U8, f"w1_sb{e}") for e in range(E)]
-        w3_sb = [held([P, PASSES * 2 * H], U8, f"w3_sb{e}") for e in range(E)]
+        w1_sb = [held([P, PASSES * 2 * H], U8, f"w1_sb{e}") for e in range(2, E)]
+        w3_sb = [held([P, PASSES * 2 * H], U8, f"w3_sb{e}") for e in range(2, E)]
         w2_sb = held([P, E * 2 * N], U8, "w2_sb")
         w1_pl = [held([P, (hi - lo) * PASSES * H], U8, f"w1_pl{lo}") for lo, hi in SCALE_GROUPS]
         w3_pl = [held([P, (hi - lo) * PASSES * H], U8, f"w3_pl{lo}") for lo, hi in SCALE_GROUPS]
         w2_pl = held([P, E * N], U8, "w2_pl")
         gate_sb = held([P, 2 * T], F32, "gate_sb")
-        xg = [held([P, 6 * TILE], U32, f"xg{o}") for o in range(PASSES)]
+        xg = held([P, 15 * TILE], U32, "xg")
+        first_sb = [[held([P, 2 * 2 * H], U8, f"first_sb{m}{o}") for o in range(PASSES)] for m in range(2)]
         xs_first = held([P, 10 * TILE], U8, "xs_first")
         xs_second = [held([P, 4 * TILE], U8, f"xs_second{c}") for c in range(3)]
         y_sb = held([P, S], F32, "y_sb")
@@ -86,9 +87,20 @@ def tile_moe_pkd_glu_silu_kernel(
 
         def load_words(m, e):
             nc.sync.dma_start(
-                out=(w1_sb, w3_sb)[m][e][:].bitcast(I32).rearrange("p (s b) -> p s b", s=PASSES),
+                out=(w1_sb, w3_sb)[m][e - 2][:].bitcast(I32).rearrange("p (s b) -> p s b", s=PASSES),
                 in_=(w1_words, w3_words)[m][e].rearrange("s p b -> p s b").bitcast(I32),
             )
+
+        def load_first(m, o):
+            nc.sync.dma_start(
+                out=first_sb[m][o][:].bitcast(I32).rearrange("p (e b) -> p e b", e=2),
+                in_=(w1_words, w3_words)[m][0:2, o].rearrange("e p b -> p e b").bitcast(I32),
+            )
+
+        def weights(e, m, o):
+            if e < 2:
+                return first_sb[m][o][:, e * 2 * H : (e + 1) * 2 * H]
+            return (w1_sb, w3_sb)[m][e - 2][:, o * 2 * H : (o + 1) * 2 * H]
 
         zero(nc.gpsimd, xs_win[:])
         zero(nc.gpsimd, w3_pl[0][:])
@@ -117,14 +129,14 @@ def tile_moe_pkd_glu_silu_kernel(
         def load_tokens(o):
             nc.sync.dma_start(out=xw_win[o][:], in_=x_words[o].rearrange("p t r -> p (t r)").bitcast(I32))
 
-        def word_col(g):
-            return WORD_TILES[g] * TILE
+        def word_col(g, o):
+            return WORD_TILES[o][g] * TILE
 
         def gather_words(o, g0, g1):
             window = xw_win[o][:].bitcast(U32)
-            col = word_col(g0)
+            col = word_col(g0, o)
             nc.vector.tensor_copy(
-                xg[o][:, col : col + (g1 - g0) * TILE], window.indirect(slots(g0 * TILE, g1 * TILE))
+                xg[:, col : col + (g1 - g0) * TILE], window.indirect(slots(g0 * TILE, g1 * TILE))
             )
 
         def token_scales(e, o, j):
@@ -137,9 +149,9 @@ def tile_moe_pkd_glu_silu_kernel(
             col = ((e - SCALE_GROUPS[grp][0]) * PASSES + o) * H
             nc.tensor.matmul_mx(
                 out=up_bank(g, m)[:],
-                lhsT=xg[o][:, word_col(g) : word_col(g) + TILE].bitcast(FP8X4),
+                lhsT=xg[:, word_col(g, o) : word_col(g, o) + TILE].bitcast(FP8X4),
                 lhsT_scale=token_scales(e, o, j),
-                rhs=(w1_sb, w3_sb)[m][e][:, o * 2 * H : (o + 1) * 2 * H].bitcast(FP4X4),
+                rhs=weights(e, m, o).bitcast(FP4X4),
                 rhs_scale=(w1_pl, w3_pl)[m][grp][:, col : col + H],
                 start=(o == 0),
                 stop=(o == PASSES - 1),
@@ -207,12 +219,11 @@ def tile_moe_pkd_glu_silu_kernel(
 
         gather_bytes(0)
         load_tokens(0)
-        load_words(0, 0)
+        load_first(0, 0)
         load_scales(nc.sync, 0, 0)
-        load_words(1, 0)
-        load_plane(nc.sync, w3_pl[0], w3_scales, *SCALE_GROUPS[0], range(1))
         load_tokens(1)
-        load_plane(nc.sync, w3_pl[0], w3_scales, *SCALE_GROUPS[0], range(1, 2))
+        load_first(1, 0)
+        load_plane(nc.sync, w3_pl[0], w3_scales, *SCALE_GROUPS[0], range(2))
         move_bytes(0)
         load_plane(nc.gpsimd, w3_pl[0], w3_scales, *SCALE_GROUPS[0], range(2, 4))
         zero(nc.gpsimd, xs_second[2][:])
@@ -221,8 +232,8 @@ def tile_moe_pkd_glu_silu_kernel(
         zero(nc.gpsimd, w3_pl[2][:])
         zero(nc.gpsimd, w2_pl[:])
         make_identity(nc, ident[:])
-        load_words(1, 1)
-        load_words(0, 1)
+        load_first(0, 1)
+        load_first(1, 1)
         load_scales(nc.sync, 0, 1)
         load_words(1, 2)
         load_words(0, 2)
@@ -230,19 +241,21 @@ def tile_moe_pkd_glu_silu_kernel(
 
         gather_words(0, 0, 1)
         gather_words(0, 1, 2)
+        gather_words(0, 2, 4)
         gather_words(1, 0, 2)
-        for o in range(PASSES):
-            gather_words(o, 2, 4)
+        gather_words(1, 2, 4)
         for m in range(2):
-            for g in range(2):
+            for g in range(SHARED):
                 up_pass(g, m, 0)
         gather_bytes(1)
         move_bytes(1)
-        gather_words(0, 4, 8)
-        for g in range(2):
+        for g in range(SHARED):
             for m in range(2):
                 up_pass(g, m, 1)
+        gather_words(0, 4, 8)
         gather_words(1, 4, 8)
+        for o in range(PASSES):
+            gather_words(o, 8, 10)
         load_words(1, 3)
         load_words(0, 3)
         load_scales(nc.sync, 0, 2)
@@ -250,10 +263,10 @@ def tile_moe_pkd_glu_silu_kernel(
         load_words(0, 4)
         load_scales(nc.sync, 1, 2)
 
-        gated(0)
-        gated(1)
+        for g in range(SHARED):
+            gated(g)
 
-        for g in range(2, TILES - 2):
+        for g in range(SHARED, TILES - 2):
             if g in (4, 8):
                 for m in range(2):
                     for tile in (g, g + 1):
@@ -270,10 +283,8 @@ def tile_moe_pkd_glu_silu_kernel(
                 for m in range(2):
                     for o in range(PASSES):
                         up_pass(g, m, o)
-            if g == 3:
+            if g == 4:
                 gather_bytes(2)
-                for o in range(PASSES):
-                    gather_words(o, 8, 10)
                 move_bytes(2)
                 load_words(1, 5)
                 load_words(0, 5)

@@ -28,7 +28,8 @@ SCALE_GROUPS = ((0, 2), (2, 4), (4, 6))
 BYTE_COLS = (6 * TILE, 3 * TILE, 0)
 WORD_TILES = ((0, 1, 2, 3, 3, 4, 5, 6, 11, 12, 5, 6), (10, 11, 12, 13, 7, 8, 9, 10, 13, 14, 9, 10))
 SHARED = 4
-OUT_CHUNKS = ((0, 384), (384, 640), (640, 768))
+TURNED = 256
+OUT_CHUNKS = ((256, 512), (512, 640), (640, 768))
 
 
 def group_of(groups, e):
@@ -112,7 +113,7 @@ def tile_moe_pkd_glu_silu_kernel(
         nc.sync.dma_start(offs_sb[:], offs)
         token_rows = x_scales.rearrange("o (q r) t -> r q o t", r=4)
         for r in range(4):
-            (nc.scalar, nc.sync)[r // 2].dma_start(out=xs_win[r:P:16, :].bitcast(I32), in_=token_rows[r].bitcast(I32))
+            nc.sync.dma_start(out=xs_win[r:P:16, :].bitcast(I32), in_=token_rows[r].bitcast(I32))
 
         def slots(lo, hi):
             return offs_sb[:, lo // LIST : hi // LIST]
@@ -172,6 +173,14 @@ def tile_moe_pkd_glu_silu_kernel(
                 lin = held([P, H], F32, f"lin{g}")
                 nc.scalar.copy(lin[:].rearrange("s (u p d) -> s u p d", u=2, d=2), by_word_half(up_bank(g, 1)))
                 nc.gpsimd.tensor_tensor(h[:], lin[:], act[:], MULT)
+            elif g == TILES - 1:
+                for u in range(2):
+                    nc.vector.tensor_tensor(
+                        h[:].rearrange("s (u p d) -> s u p d", u=2, d=2)[:, u],
+                        by_word_half(up_bank(g, 1))[:, u],
+                        act[:].rearrange("s (u p d) -> s u p d", u=2, d=2)[:, u],
+                        MULT,
+                    )
             else:
                 nc.vector.tensor_tensor(
                     h[:].rearrange("s (u p d) -> s u p d", u=2, d=2),
@@ -183,7 +192,9 @@ def tile_moe_pkd_glu_silu_kernel(
 
         packed = {}
 
-        def turn(tiles, bank):
+        turned = {}
+
+        def turn(tiles, bank, copy_out=nc.scalar.copy):
             width = len(tiles) * TILE
             for j, g in enumerate(tiles):
                 words = h_tiles[g][:].bitcast(F32)
@@ -191,14 +202,18 @@ def tile_moe_pkd_glu_silu_kernel(
                     col = (2 * j + u) * TILE
                     nc.tensor.transpose(bank[:, col : col + TILE], words[:, u * P : (u + 1) * P], ident[:])
             h_turned = held([P, 4 * width], BF16, f"h_turned{tiles[0]}")
-            nc.scalar.copy(
+            copy_out(
                 h_turned[:].bitcast(F32).rearrange("p (j s u) -> p j s u", u=2, s=TILE),
                 bank[:, : 2 * width].rearrange("p (j u s) -> p j s u", u=2, s=TILE),
             )
-            codes = held([P, width], U32, f"codes{tiles[0]}")
-            h_scales = held([P, width], U8, f"h_scales{tiles[0]}")
+            turned[tiles[0]] = (h_turned, width)
+
+        def quantize(first):
+            h_turned, width = turned[first]
+            codes = held([P, width], U32, f"codes{first}")
+            h_scales = held([P, width], U8, f"h_scales{first}")
             nc.vector.quantize_mx(out=codes[:].bitcast(FP8X4), scales=h_scales[:], in_=h_turned[:])
-            packed[tiles[0]] = (codes, h_scales, width)
+            packed[first] = (codes, h_scales, width)
 
         def down(firsts, bank, copy_out):
             col = 0
@@ -307,6 +322,8 @@ def tile_moe_pkd_glu_silu_kernel(
                 turn([2, 3], up_bank(9, 0))
                 turn([4, 5], up_bank(8, 1))
                 turn([6, 7], up_bank(9, 1))
+                for first in (0, 2, 4, 6):
+                    quantize(first)
 
         for m in range(2):
             for g in (10, 11):
@@ -315,13 +332,15 @@ def tile_moe_pkd_glu_silu_kernel(
         gated(10)
         gated(11)
         turn([8, 9], up_bank(10, 0))
-        down([0, 2], up_bank(10, 1), nc.vector.tensor_copy)
-        turn([10], up_bank(9, 0))
+        turn([10], up_bank(9, 0), nc.vector.tensor_copy)
         turn([11], up_bank(8, 0))
-        down([4, 6], up_bank(11, 1), nc.scalar.copy)
-        down([8], up_bank(9, 1), nc.scalar.copy)
-        down([10], up_bank(8, 1), nc.scalar.copy)
-        down([11], up_bank(11, 0), nc.scalar.copy)
+        for first in (8, 10, 11):
+            quantize(first)
+        down([0, 2], up_bank(11, 1), nc.scalar.copy)
+        down([4, 6], up_bank(10, 1), nc.scalar.copy)
+        down([8], up_bank(9, 1), nc.vector.tensor_copy)
+        down([10], up_bank(8, 1), nc.vector.tensor_copy)
+        down([11], up_bank(11, 0), nc.vector.tensor_copy)
 
         parts = [held([P, T], F32, f"part{r}") for r in range(2)]
 
@@ -334,7 +353,29 @@ def tile_moe_pkd_glu_silu_kernel(
                 MULT,
             )
 
-        weighted(0, 0, T)
+        for r in range(2):
+            weighted(r, 0, TURNED)
+        blocks = range(TURNED // P)
+        for r in range(2):
+            for j in blocks:
+                nc.tensor.matmul(
+                    banks[j][:, :P],
+                    lhsT=parts[r][:, j * P : (j + 1) * P],
+                    rhs=ident[:],
+                    start=(r == 0),
+                    stop=(r == 1),
+                    is_transpose=True,
+                )
+        first_total = held([P, TURNED], F32, "first_total")
+        for j in blocks:
+            by_token = held([P, P], F32, f"by_token{j}")
+            nc.scalar.copy(by_token[:], banks[j][:, :P])
+            nc.tensor.transpose(banks[4 + j][:, :P], by_token[:], ident[:])
+        for j in blocks:
+            nc.scalar.copy(first_total[:, j * P : (j + 1) * P], banks[4 + j][:, :P])
+        nc.scalar.dma_start(out=out[:, :TURNED], in_=first_total[:])
+
+        weighted(0, TURNED, T)
         weighted(1, *OUT_CHUNKS[0])
         for c, (lo, hi) in enumerate(OUT_CHUNKS):
             if c + 1 < len(OUT_CHUNKS):

@@ -26,10 +26,9 @@ TILES = S // TILE
 LIST = 16
 SCALE_GROUPS = ((0, 2), (2, 4), (4, 6))
 BYTE_COLS = (6 * TILE, 3 * TILE, 0)
-WORD_TILES = ((0, 1, 2, 3, 3, 4, 5, 6, 11, 12, 5, 6), (10, 11, 12, 13, 7, 8, 9, 10, 13, 14, 9, 10))
+WORD_TILES = ((0, 1, 2, 3, 3, 4, 5, 6, 11, 12, 4, 5), (10, 11, 12, 13, 7, 8, 9, 10, 13, 14, 9, 10))
 SHARED = 4
-TURNED = 256
-OUT_CHUNKS = ((256, 512), (512, 640), (640, 768))
+OUT_CHUNKS = ((0, 384), (384, 640), (640, 768))
 
 
 def group_of(groups, e):
@@ -63,7 +62,8 @@ def tile_moe_pkd_glu_silu_kernel(
         w2_pl = held([P, E * N], U8, "w2_pl")
         gate_sb = held([P, 2 * T], F32, "gate_sb")
         xg = held([P, 15 * TILE], U32, "xg")
-        first_sb = [[held([P, 2 * 2 * H], U8, f"first_sb{m}{o}") for o in range(PASSES)] for m in range(2)]
+        first_sb = {(m, o): held([P, 2 * 2 * H], U8, f"first_sb{m}{o}") for m, o in ((1, 0), (0, 1), (1, 1))}
+        lead_sb = [held([P, 2 * H], U8, f"lead_sb{e}") for e in range(2)]
         xs_first = held([P, 10 * TILE], U8, "xs_first")
         xs_second = [held([P, 4 * TILE], U8, f"xs_second{c}") for c in range(3)]
         y_sb = held([P, S], F32, "y_sb")
@@ -94,13 +94,18 @@ def tile_moe_pkd_glu_silu_kernel(
 
         def load_first(m, o):
             nc.sync.dma_start(
-                out=first_sb[m][o][:].bitcast(I32).rearrange("p (e b) -> p e b", e=2),
+                out=first_sb[m, o][:].bitcast(I32).rearrange("p (e b) -> p e b", e=2),
                 in_=(w1_words, w3_words)[m][0:2, o].rearrange("e p b -> p e b").bitcast(I32),
             )
 
+        def load_lead(e):
+            nc.sync.dma_start(out=lead_sb[e][:].bitcast(I32), in_=w1_words[e, 0].bitcast(I32))
+
         def weights(e, m, o):
+            if e < 2 and m == 0 and o == 0:
+                return lead_sb[e][:]
             if e < 2:
-                return first_sb[m][o][:, e * 2 * H : (e + 1) * 2 * H]
+                return first_sb[m, o][:, e * 2 * H : (e + 1) * 2 * H]
             return (w1_sb, w3_sb)[m][e - 2][:, o * 2 * H : (o + 1) * 2 * H]
 
         zero(nc.gpsimd, xs_win[:])
@@ -234,15 +239,16 @@ def tile_moe_pkd_glu_silu_kernel(
 
         gather_bytes(0)
         load_tokens(0)
-        load_first(0, 0)
+        load_lead(0)
         load_scales(nc.sync, 0, 0)
+        load_lead(1)
         load_tokens(1)
         load_first(1, 0)
         load_plane(nc.sync, w3_pl[0], w3_scales, *SCALE_GROUPS[0], range(2))
         move_bytes(0)
-        load_plane(nc.gpsimd, w3_pl[0], w3_scales, *SCALE_GROUPS[0], range(2, 4))
         zero(nc.gpsimd, xs_second[2][:])
         zero(nc.gpsimd, w3_pl[1][:])
+        load_plane(nc.gpsimd, w3_pl[0], w3_scales, *SCALE_GROUPS[0], range(2, 4))
         zero(nc.gpsimd, w1_pl[2][:])
         zero(nc.gpsimd, w3_pl[2][:])
         zero(nc.gpsimd, w2_pl[:])
@@ -314,12 +320,11 @@ def tile_moe_pkd_glu_silu_kernel(
                     out=gate_sb[:].rearrange("n (r t) -> n r t", r=2), in_=gate.rearrange("r n t -> n r t")
                 )
             gated(g)
-            if g == 7:
-                for o in range(PASSES):
-                    gather_words(o, 10, 12)
+            if g in (6, 7):
+                gather_words(g - 6, 10, 12)
             if g == 9:
                 turn([0, 1], up_bank(8, 0))
-                turn([2, 3], up_bank(9, 0))
+                turn([2, 3], up_bank(9, 0), nc.vector.tensor_copy)
                 turn([4, 5], up_bank(8, 1))
                 turn([6, 7], up_bank(9, 1))
                 for first in (0, 2, 4, 6):
@@ -353,29 +358,7 @@ def tile_moe_pkd_glu_silu_kernel(
                 MULT,
             )
 
-        for r in range(2):
-            weighted(r, 0, TURNED)
-        blocks = range(TURNED // P)
-        for r in range(2):
-            for j in blocks:
-                nc.tensor.matmul(
-                    banks[j][:, :P],
-                    lhsT=parts[r][:, j * P : (j + 1) * P],
-                    rhs=ident[:],
-                    start=(r == 0),
-                    stop=(r == 1),
-                    is_transpose=True,
-                )
-        first_total = held([P, TURNED], F32, "first_total")
-        for j in blocks:
-            by_token = held([P, P], F32, f"by_token{j}")
-            nc.scalar.copy(by_token[:], banks[j][:, :P])
-            nc.tensor.transpose(banks[4 + j][:, :P], by_token[:], ident[:])
-        for j in blocks:
-            nc.scalar.copy(first_total[:, j * P : (j + 1) * P], banks[4 + j][:, :P])
-        nc.scalar.dma_start(out=out[:, :TURNED], in_=first_total[:])
-
-        weighted(0, TURNED, T)
+        weighted(0, 0, T)
         weighted(1, *OUT_CHUNKS[0])
         for c, (lo, hi) in enumerate(OUT_CHUNKS):
             if c + 1 < len(OUT_CHUNKS):

@@ -118,7 +118,7 @@ def tile_moe_pkd_glu_silu_kernel(
         nc.sync.dma_start(offs_sb[:], offs)
         token_rows = x_scales.rearrange("o (q r) t -> r q o t", r=4)
         for r in range(4):
-            nc.sync.dma_start(out=xs_win[r:P:16, :].bitcast(I32), in_=token_rows[r].bitcast(I32))
+            (nc.scalar, nc.sync)[r // 2].dma_start(out=xs_win[r:P:16, :].bitcast(I32), in_=token_rows[r].bitcast(I32))
 
         def slots(lo, hi):
             return offs_sb[:, lo // LIST : hi // LIST]
@@ -240,7 +240,8 @@ def tile_moe_pkd_glu_silu_kernel(
         gather_bytes(0)
         load_tokens(0)
         load_lead(0)
-        load_scales(nc.sync, 0, 0)
+        load_plane(nc.scalar, w1_pl[0], w1_scales, *SCALE_GROUPS[0], range(1))
+        load_plane(nc.sync, w1_pl[0], w1_scales, *SCALE_GROUPS[0], range(1, 4))
         load_lead(1)
         load_tokens(1)
         load_first(1, 0)

@@ -18,6 +18,7 @@ FP4X4 = mybir.dt.float4_e2m1fn_x4
 MULT = mybir.AluOpType.mult
 ADD = mybir.AluOpType.add
 SILU = mybir.ActivationFunctionType.Silu
+COPY = mybir.ActivationFunctionType.Copy
 
 P = 128
 PASSES = 2
@@ -28,7 +29,7 @@ SCALE_GROUPS = ((0, 2), (2, 4), (4, 6))
 BYTE_COLS = (6 * TILE, 3 * TILE, 0)
 WORD_TILES = ((0, 1, 2, 3, 3, 4, 5, 6, 11, 12, 4, 5), (10, 11, 12, 13, 7, 8, 9, 10, 13, 14, 9, 10))
 SHARED = 4
-OUT_CHUNKS = ((0, 384), (384, 640), (640, 768))
+PIECES = ((0, 128), (128, 384), (384, 640), (640, 768))
 
 
 def group_of(groups, e):
@@ -60,7 +61,7 @@ def tile_moe_pkd_glu_silu_kernel(
         w1_pl = [held([P, (hi - lo) * PASSES * H], U8, f"w1_pl{lo}") for lo, hi in SCALE_GROUPS]
         w3_pl = [held([P, (hi - lo) * PASSES * H], U8, f"w3_pl{lo}") for lo, hi in SCALE_GROUPS]
         w2_pl = held([P, E * N], U8, "w2_pl")
-        gate_sb = held([P, 2 * T], F32, "gate_sb")
+        gate_sb = held([P, 2, T], F32, "gate_sb")
         xg = held([P, 15 * TILE], U32, "xg")
         first_sb = {(m, o): held([P, 2 * 2 * H], U8, f"first_sb{m}{o}") for m, o in ((1, 0), (0, 1), (1, 1))}
         lead_sb = [held([P, 2 * H], U8, f"lead_sb{e}") for e in range(2)]
@@ -317,9 +318,7 @@ def tile_moe_pkd_glu_silu_kernel(
                 )
                 nc.sync.dma_start(pos1_sb[:], pos1)
                 nc.sync.dma_start(pos2_sb[:], pos2)
-                nc.sync.dma_start(
-                    out=gate_sb[:].rearrange("n (r t) -> n r t", r=2), in_=gate.rearrange("r n t -> n r t")
-                )
+                nc.sync.dma_start(out=gate_sb[:], in_=gate.rearrange("r n t -> n r t"))
             gated(g)
             if g in (6, 7):
                 gather_words(g - 6, 10, 12)
@@ -348,22 +347,39 @@ def tile_moe_pkd_glu_silu_kernel(
         down([10], up_bank(8, 1), nc.vector.tensor_copy)
         down([11], up_bank(11, 0), nc.vector.tensor_copy)
 
-        parts = [held([P, T], F32, f"part{r}") for r in range(2)]
+        def chosen(r, lo, hi):
+            return y_sb[:].indirect((pos1_sb, pos2_sb)[r][:, lo // LIST : hi // LIST])
 
-        def weighted(r, lo, hi):
-            pos_sb = (pos1_sb, pos2_sb)[r]
-            nc.vector.tensor_tensor(
-                parts[r][:, lo:hi],
-                y_sb[:].indirect(pos_sb[:, lo // LIST : hi // LIST]),
-                gate_sb[:, r * T + lo : r * T + hi],
-                MULT,
-            )
+        split = PIECES[0][1]
+        firsts = held([P, T - split], F32, "firsts")
+        nc.vector.tensor_tensor(firsts[:], chosen(0, split, T), gate_sb[:, 0, split:T], MULT)
+        both = held([P, 2, split], F32, "both")
+        for r in range(2):
+            nc.scalar.activation(both[:, r, :], chosen(r, 0, split), COPY)
+        plain = [both]
+        for lo, hi in PIECES[1:]:
+            plain.append(held([P, hi - lo], F32, f"plain{lo}"))
+            nc.scalar.activation(plain[-1][:], chosen(1, lo, hi), COPY)
 
-        weighted(0, 0, T)
-        weighted(1, *OUT_CHUNKS[0])
-        for c, (lo, hi) in enumerate(OUT_CHUNKS):
-            if c + 1 < len(OUT_CHUNKS):
-                weighted(1, *OUT_CHUNKS[c + 1])
-            total = held([P, hi - lo], F32, f"total{c}")
-            nc.vector.tensor_tensor(total[:], parts[0][:, lo:hi], parts[1][:, lo:hi], ADD)
+        weighted = []
+
+        def weigh(i):
+            lo, hi = PIECES[i]
+            weighted.append(held(plain[i].shape, F32, f"weighted{lo}"))
+            factor = gate_sb[:, :, lo:hi] if i == 0 else gate_sb[:, 1, lo:hi]
+            nc.vector.tensor_tensor(weighted[i][:], plain[i][:], factor, MULT)
+
+        def finish(i):
+            lo, hi = PIECES[i]
+            total = held([P, hi - lo], F32, f"total{lo}")
+            if i == 0:
+                nc.vector.tensor_tensor(total[:], weighted[i][:, 0, :], weighted[i][:, 1, :], ADD)
+            else:
+                nc.vector.tensor_tensor(total[:], firsts[:, lo - split : hi - split], weighted[i][:], ADD)
             nc.sync.dma_start(out=out[:, lo:hi], in_=total[:])
+
+        for i in range(0, len(PIECES), 2):
+            weigh(i)
+            weigh(i + 1)
+            finish(i)
+            finish(i + 1)

@@ -26,7 +26,7 @@ TILE = 128
 TILES = S // TILE
 LIST = 16
 SCALE_GROUPS = ((0, 2), (2, 4), (4, 6))
-BYTE_COLS = (6 * TILE, 3 * TILE, 0)
+BYTE_TAGS = (None, "lead_sb0", "first_sb01")
 WORD_TILES = ((0, 1, 2, 3, 3, 4, 5, 6, 11, 12, 4, 5), (10, 11, 12, 13, 7, 8, 9, 10, 13, 14, 9, 10))
 SHARED = 4
 PIECES = ((0, 128), (128, 384), (384, 640), (640, 768))
@@ -44,8 +44,8 @@ def tile_moe_pkd_glu_silu_kernel(
         keep = ctx.enter_context(tc.tile_pool(name="keep", bufs=1))
         psum = ctx.enter_context(tc.psum_pool(name="psum", bufs=1))
 
-        def held(shape, dtype, name):
-            return keep.tile(shape, dtype, name=name, align_bytes=256)
+        def held(shape, dtype, name, tag=None):
+            return keep.tile(shape, dtype, name=name, tag=tag or name, align_bytes=256)
 
         def zero(engine, tile_ap):
             engine.memset(tile_ap.bitcast(I32), 0)
@@ -58,15 +58,18 @@ def tile_moe_pkd_glu_silu_kernel(
         w1_sb = [held([P, PASSES * 2 * H], U8, f"w1_sb{e}") for e in range(2, E)]
         w3_sb = [held([P, PASSES * 2 * H], U8, f"w3_sb{e}") for e in range(2, E)]
         w2_sb = held([P, E * 2 * N], U8, "w2_sb")
-        w1_pl = [held([P, (hi - lo) * PASSES * H], U8, f"w1_pl{lo}") for lo, hi in SCALE_GROUPS]
-        w3_pl = [held([P, (hi - lo) * PASSES * H], U8, f"w3_pl{lo}") for lo, hi in SCALE_GROUPS]
+        w1_pl = [held([P, (hi - lo) * PASSES * H], U8, f"w1_pl{lo}") for lo, hi in SCALE_GROUPS[:2]]
+        w3_pl = [held([P, (hi - lo) * PASSES * H], U8, f"w3_pl{lo}") for lo, hi in SCALE_GROUPS[:2]]
+        w1_pl.append(w1_pl[0])
+        w3_pl.append(w3_pl[0])
         w2_pl = held([P, E * N], U8, "w2_pl")
         gate_sb = held([P, 2, T], F32, "gate_sb")
         xg = held([P, 15 * TILE], U32, "xg")
         first_sb = {(m, o): held([P, 2 * 2 * H], U8, f"first_sb{m}{o}") for m, o in ((1, 0), (0, 1), (1, 1))}
         lead_sb = [held([P, 2 * H], U8, f"lead_sb{e}") for e in range(2)]
-        xs_first = held([P, 10 * TILE], U8, "xs_first")
-        xs_second = [held([P, 4 * TILE], U8, f"xs_second{c}") for c in range(3)]
+        xs_first = {}
+        xs_second = [held([P, 4 * TILE], U8, f"xs_second{c}") for c in range(2)]
+        xs_second.append(xs_second[0])
         y_sb = held([P, S], F32, "y_sb")
         ident = held([P, P], F32, "ident")
 
@@ -115,6 +118,7 @@ def tile_moe_pkd_glu_silu_kernel(
         zero(nc.vector, xs_second[0][:])
         zero(nc.vector, xs_second[1][:])
         zero(nc.vector, w1_pl[1][:])
+        zero(nc.vector, w3_pl[1][:])
 
         nc.sync.dma_start(offs_sb[:], offs)
         token_rows = x_scales.rearrange("o (q r) t -> r q o t", r=4)
@@ -125,13 +129,14 @@ def tile_moe_pkd_glu_silu_kernel(
             return offs_sb[:, lo // LIST : hi // LIST]
 
         def byte_cols(c):
-            return xs_first[:, BYTE_COLS[c] : BYTE_COLS[c] + 4 * TILE]
+            return xs_first[c][:]
 
         def gather_bytes(c):
+            xs_first[c] = held([P, 4 * TILE], U8, f"xs_first{c}", BYTE_TAGS[c])
             nc.vector.tensor_copy(byte_cols(c), xs_win[:].indirect(slots(c * 4 * TILE, (c + 1) * 4 * TILE)))
 
-        def move_bytes(c):
-            nc.sync.dma_start(out=xs_second[c][0:112, :].bitcast(I32), in_=byte_cols(c)[16:P, :].bitcast(I32))
+        def move_bytes(c, queue=nc.sync):
+            queue.dma_start(out=xs_second[c][0:112, :].bitcast(I32), in_=byte_cols(c)[16:P, :].bitcast(I32))
 
         def load_tokens(o):
             nc.sync.dma_start(out=xw_win[o][:], in_=x_words[o].rearrange("p t r -> p (t r)").bitcast(I32))
@@ -148,7 +153,7 @@ def tile_moe_pkd_glu_silu_kernel(
 
         def token_scales(e, o, j):
             c, place = divmod(2 * e + j, 4)
-            return (byte_cols(c), xs_second[c])[o][:, place * TILE : (place + 1) * TILE]
+            return (xs_first[c], xs_second[c])[o][:, place * TILE : (place + 1) * TILE]
 
         def up_pass(g, m, o):
             e, j = divmod(g, 2)
@@ -247,13 +252,9 @@ def tile_moe_pkd_glu_silu_kernel(
         load_tokens(1)
         load_first(1, 0)
         load_plane(nc.sync, w3_pl[0], w3_scales, *SCALE_GROUPS[0], range(2))
-        move_bytes(0)
-        zero(nc.gpsimd, xs_second[2][:])
-        zero(nc.gpsimd, w3_pl[1][:])
-        load_plane(nc.gpsimd, w3_pl[0], w3_scales, *SCALE_GROUPS[0], range(2, 4))
-        zero(nc.gpsimd, w1_pl[2][:])
-        zero(nc.gpsimd, w3_pl[2][:])
         zero(nc.gpsimd, w2_pl[:])
+        load_plane(nc.gpsimd, w3_pl[0], w3_scales, *SCALE_GROUPS[0], range(2, 4))
+        move_bytes(0, nc.gpsimd)
         make_identity(nc, ident[:])
         load_first(0, 1)
         load_first(1, 1)
@@ -277,6 +278,7 @@ def tile_moe_pkd_glu_silu_kernel(
                 up_pass(g, m, 1)
         gather_words(0, 4, 8)
         gather_words(1, 4, 8)
+        gather_bytes(2)
         for o in range(PASSES):
             gather_words(o, 8, 10)
         load_words(1, 3)
@@ -307,7 +309,6 @@ def tile_moe_pkd_glu_silu_kernel(
                     for o in range(PASSES):
                         up_pass(g, m, o)
             if g == 4:
-                gather_bytes(2)
                 move_bytes(2)
                 load_words(1, 5)
                 load_words(0, 5)

@@ -26,10 +26,10 @@ TILE = 128
 TILES = S // TILE
 LIST = 16
 SCALE_GROUPS = ((0, 2), (2, 4), (4, 6))
-BYTE_TAGS = (None, "lead_sb0", "first_sb01")
-WORD_TILES = ((0, 1, 2, 3, 3, 4, 5, 6, 11, 12, 4, 5), (10, 11, 12, 13, 7, 8, 9, 10, 13, 14, 9, 10))
+BYTE_TAGS = (None, "lead_sb1", "pair_sb")
+WORD_TILES = ((2, 3, 0, 1, 3, 4, 5, 6, 11, 12, 4, 5), (10, 11, 12, 13, 7, 8, 9, 10, 13, 14, 9, 10))
 SHARED = 4
-PIECES = ((0, 128), (128, 384), (384, 640), (640, 768))
+PIECES = ((0, 128), (128, 448), (448, 640), (640, 768))
 
 
 def group_of(groups, e):
@@ -55,17 +55,17 @@ def tile_moe_pkd_glu_silu_kernel(
         pos2_sb = held([P, T // LIST], U16, "pos2_sb")
         xs_win = held([P, T], U8, "xs_win")
         xw_win = [held([P, T], I32, f"xw_win{o}") for o in range(PASSES)]
-        w1_sb = [held([P, PASSES * 2 * H], U8, f"w1_sb{e}") for e in range(2, E)]
-        w3_sb = [held([P, PASSES * 2 * H], U8, f"w3_sb{e}") for e in range(2, E)]
+        w1_sb = {e: held([P, PASSES * 2 * H], U8, f"w1_sb{e}") for e in range(2, E)}
+        w3_sb = [held([P, PASSES * 2 * H], U8, f"w3_sb{e}") for e in range(E)]
         w2_sb = held([P, E * 2 * N], U8, "w2_sb")
         w1_pl = [held([P, (hi - lo) * PASSES * H], U8, f"w1_pl{lo}") for lo, hi in SCALE_GROUPS[:2]]
-        w3_pl = [held([P, (hi - lo) * PASSES * H], U8, f"w3_pl{lo}") for lo, hi in SCALE_GROUPS[:2]]
         w1_pl.append(w1_pl[0])
+        w3_pl = [held([P, (hi - lo) * PASSES * H], U8, f"w3_pl{lo}") for lo, hi in SCALE_GROUPS[:2]]
         w3_pl.append(w3_pl[0])
         w2_pl = held([P, E * N], U8, "w2_pl")
         gate_sb = held([P, 2, T], F32, "gate_sb")
         xg = held([P, 15 * TILE], U32, "xg")
-        first_sb = {(m, o): held([P, 2 * 2 * H], U8, f"first_sb{m}{o}") for m, o in ((1, 0), (0, 1), (1, 1))}
+        pair_sb = held([P, 2 * 2 * H], U8, "pair_sb")
         lead_sb = [held([P, 2 * H], U8, f"lead_sb{e}") for e in range(2)]
         xs_first = {}
         xs_second = [held([P, 4 * TILE], U8, f"xs_second{c}") for c in range(2)]
@@ -92,14 +92,14 @@ def tile_moe_pkd_glu_silu_kernel(
 
         def load_words(m, e):
             nc.sync.dma_start(
-                out=(w1_sb, w3_sb)[m][e - 2][:].bitcast(I32).rearrange("p (s b) -> p s b", s=PASSES),
+                out=(w1_sb, w3_sb)[m][e][:].bitcast(I32).rearrange("p (s b) -> p s b", s=PASSES),
                 in_=(w1_words, w3_words)[m][e].rearrange("s p b -> p s b").bitcast(I32),
             )
 
-        def load_first(m, o):
+        def load_pair():
             nc.sync.dma_start(
-                out=first_sb[m, o][:].bitcast(I32).rearrange("p (e b) -> p e b", e=2),
-                in_=(w1_words, w3_words)[m][0:2, o].rearrange("e p b -> p e b").bitcast(I32),
+                out=pair_sb[:].bitcast(I32).rearrange("p (e b) -> p e b", e=2),
+                in_=w1_words[0:2, 1].rearrange("e p b -> p e b").bitcast(I32),
             )
 
         def load_lead(e):
@@ -108,9 +108,9 @@ def tile_moe_pkd_glu_silu_kernel(
         def weights(e, m, o):
             if e < 2 and m == 0 and o == 0:
                 return lead_sb[e][:]
-            if e < 2:
-                return first_sb[m, o][:, e * 2 * H : (e + 1) * 2 * H]
-            return (w1_sb, w3_sb)[m][e - 2][:, o * 2 * H : (o + 1) * 2 * H]
+            if e < 2 and m == 0:
+                return pair_sb[:, e * 2 * H : (e + 1) * 2 * H]
+            return (w1_sb, w3_sb)[m][e][:, o * 2 * H : (o + 1) * 2 * H]
 
         zero(nc.gpsimd, xs_win[:])
         zero(nc.gpsimd, w3_pl[0][:])
@@ -135,8 +135,8 @@ def tile_moe_pkd_glu_silu_kernel(
             xs_first[c] = held([P, 4 * TILE], U8, f"xs_first{c}", BYTE_TAGS[c])
             nc.vector.tensor_copy(byte_cols(c), xs_win[:].indirect(slots(c * 4 * TILE, (c + 1) * 4 * TILE)))
 
-        def move_bytes(c, queue=nc.sync):
-            queue.dma_start(out=xs_second[c][0:112, :].bitcast(I32), in_=byte_cols(c)[16:P, :].bitcast(I32))
+        def move_bytes(c):
+            nc.sync.dma_start(out=xs_second[c][0:112, :].bitcast(I32), in_=byte_cols(c)[16:P, :].bitcast(I32))
 
         def load_tokens(o):
             nc.sync.dma_start(out=xw_win[o][:], in_=x_words[o].rearrange("p t r -> p (t r)").bitcast(I32))
@@ -248,34 +248,38 @@ def tile_moe_pkd_glu_silu_kernel(
         load_lead(0)
         load_plane(nc.scalar, w1_pl[0], w1_scales, *SCALE_GROUPS[0], range(1))
         load_plane(nc.sync, w1_pl[0], w1_scales, *SCALE_GROUPS[0], range(1, 4))
-        load_lead(1)
         load_tokens(1)
-        load_first(1, 0)
+        load_lead(1)
+        load_words(1, 0)
         load_plane(nc.sync, w3_pl[0], w3_scales, *SCALE_GROUPS[0], range(2))
+        load_pair()
+        move_bytes(0)
+        load_words(1, 1)
         zero(nc.gpsimd, w2_pl[:])
         load_plane(nc.gpsimd, w3_pl[0], w3_scales, *SCALE_GROUPS[0], range(2, 4))
-        move_bytes(0, nc.gpsimd)
         make_identity(nc, ident[:])
-        load_first(0, 1)
-        load_first(1, 1)
         load_scales(nc.sync, 0, 1)
         load_words(1, 2)
         load_words(0, 2)
-        load_scales(nc.sync, 1, 1)
 
         gather_words(0, 0, 1)
         gather_words(0, 1, 2)
         gather_words(0, 2, 4)
         gather_words(1, 0, 2)
         gather_words(1, 2, 4)
-        for m in range(2):
-            for g in range(SHARED):
-                up_pass(g, m, 0)
+        for g in range(SHARED):
+            up_pass(g, 0, 0)
+        load_scales(nc.sync, 1, 1)
         gather_bytes(1)
         move_bytes(1)
-        for g in range(SHARED):
-            for m in range(2):
-                up_pass(g, m, 1)
+        for m, o in ((1, 0), (0, 1), (1, 1)):
+            for g in (0, 1):
+                up_pass(g, m, o)
+        for g in (2, 3):
+            up_pass(g, 0, 1)
+        for g in (2, 3):
+            for o in range(PASSES):
+                up_pass(g, 1, o)
         gather_words(0, 4, 8)
         gather_words(1, 4, 8)
         gather_bytes(2)

from contextlib import ExitStack

import concourse.mybir as mybir
from concourse.masks import make_identity

K, T, E, C, H, N = 1024, 768, 6, 256, 512, 128
S = E * C
FLOPS = 2 * S * (2 * K * H + H * N)

F32 = mybir.dt.float32
BF16 = mybir.dt.bfloat16
I32 = mybir.dt.int32
U32 = mybir.dt.uint32
U16 = mybir.dt.uint16
U8 = mybir.dt.uint8
FP8X4 = mybir.dt.float8_e4m3fn_x4
FP4X4 = mybir.dt.float4_e2m1fn_x4
MULT = mybir.AluOpType.mult
ADD = mybir.AluOpType.add
SILU = mybir.ActivationFunctionType.Silu
COPY = mybir.ActivationFunctionType.Copy

P = 128
PASSES = 2
TILE = 128
TILES = S // TILE
LIST = 16
SCALE_GROUPS = ((0, 2), (2, 4), (4, 6))
BYTE_TAGS = (None, "lead_sb1", "pair_sb")
WORD_TILES = ((2, 3, 0, 1, 3, 4, 5, 6, 11, 12, 4, 5), (10, 11, 12, 13, 7, 8, 9, 10, 13, 14, 9, 10))
SHARED = 4
PIECES = ((0, 128), (128, 448), (448, 640), (640, 768))


def group_of(groups, e):
    return [i for i, (lo, hi) in enumerate(groups) if lo <= e < hi][0]


def tile_moe_pkd_glu_silu_kernel(
    tc, x_words, x_scales, w1_words, w1_scales, w3_words, w3_scales, w2_words, w2_scales, gate, offs, pos1, pos2, out
):
    nc = tc.nc
    with ExitStack() as ctx:
        keep = ctx.enter_context(tc.tile_pool(name="keep", bufs=1))
        psum = ctx.enter_context(tc.psum_pool(name="psum", bufs=1))

        def held(shape, dtype, name, tag=None):
            return keep.tile(shape, dtype, name=name, tag=tag or name, align_bytes=256)

        def zero(engine, tile_ap):
            engine.memset(tile_ap.bitcast(I32), 0)

        offs_sb = held([P, S // LIST], U16, "offs_sb")
        pos1_sb = held([P, T // LIST], U16, "pos1_sb")
        pos2_sb = held([P, T // LIST], U16, "pos2_sb")
        xs_win = held([P, T], U8, "xs_win")
        xw_win = [held([P, T], I32, f"xw_win{o}") for o in range(PASSES)]
        w1_sb = {e: held([P, PASSES * 2 * H], U8, f"w1_sb{e}") for e in range(2, E)}
        w3_sb = [held([P, PASSES * 2 * H], U8, f"w3_sb{e}") for e in range(E)]
        w2_sb = held([P, E * 2 * N], U8, "w2_sb")
        w1_pl = [held([P, (hi - lo) * PASSES * H], U8, f"w1_pl{lo}") for lo, hi in SCALE_GROUPS[:2]]
        w1_pl.append(w1_pl[0])
        w3_pl = [held([P, (hi - lo) * PASSES * H], U8, f"w3_pl{lo}") for lo, hi in SCALE_GROUPS[:2]]
        w3_pl.append(w3_pl[0])
        w2_pl = held([P, E * N], U8, "w2_pl")
        gate_sb = held([P, 2, T], F32, "gate_sb")
        xg = held([P, 15 * TILE], U32, "xg")
        pair_sb = held([P, 2 * 2 * H], U8, "pair_sb")
        lead_sb = [held([P, 2 * H], U8, f"lead_sb{e}") for e in range(2)]
        xs_first = {}
        xs_second = [held([P, 4 * TILE], U8, f"xs_second{c}") for c in range(2)]
        xs_second.append(xs_second[0])
        y_sb = held([P, S], F32, "y_sb")
        ident = held([P, P], F32, "ident")

        banks = [psum.tile([P, H], F32, name=f"bank{b}") for b in range(8)]

        def up_bank(g, m):
            return banks[2 * (g % 4) + m]

        def load_plane(queue, plane, scales, lo, hi, live=range(4)):
            width = scales.shape[3]
            rows = scales[lo:hi].rearrange("e s (q r) i -> r q (e s) i", r=4)
            for r in live:
                queue.dma_start(
                    out=plane[r:P:32, :].bitcast(I32).rearrange("q (g i) -> q g i", i=width // 4),
                    in_=rows[r].bitcast(I32),
                )

        def load_scales(queue, m, grp):
            load_plane(queue, (w1_pl, w3_pl)[m][grp], (w1_scales, w3_scales)[m], *SCALE_GROUPS[grp])

        def load_words(m, e):
            nc.sync.dma_start(
                out=(w1_sb, w3_sb)[m][e][:].bitcast(I32).rearrange("p (s b) -> p s b", s=PASSES),
                in_=(w1_words, w3_words)[m][e].rearrange("s p b -> p s b").bitcast(I32),
            )

        def load_pair():
            nc.sync.dma_start(
                out=pair_sb[:].bitcast(I32).rearrange("p (e b) -> p e b", e=2),
                in_=w1_words[0:2, 1].rearrange("e p b -> p e b").bitcast(I32),
            )

        def load_lead(e):
            nc.sync.dma_start(out=lead_sb[e][:].bitcast(I32), in_=w1_words[e, 0].bitcast(I32))

        def weights(e, m, o):
            if e < 2 and m == 0 and o == 0:
                return lead_sb[e][:]
            if e < 2 and m == 0:
                return pair_sb[:, e * 2 * H : (e + 1) * 2 * H]
            return (w1_sb, w3_sb)[m][e][:, o * 2 * H : (o + 1) * 2 * H]

        zero(nc.gpsimd, xs_win[:])
        zero(nc.gpsimd, w3_pl[0][:])
        zero(nc.vector, w1_pl[0][:])
        zero(nc.vector, xs_second[0][:])
        zero(nc.vector, xs_second[1][:])
        zero(nc.vector, w1_pl[1][:])
        zero(nc.vector, w3_pl[1][:])

        nc.sync.dma_start(offs_sb[:], offs)
        token_rows = x_scales.rearrange("o (q r) t -> r q o t", r=4)
        for r in range(4):
            (nc.scalar, nc.sync)[r // 2].dma_start(out=xs_win[r:P:16, :].bitcast(I32), in_=token_rows[r].bitcast(I32))

        def slots(lo, hi):
            return offs_sb[:, lo // LIST : hi // LIST]

        def byte_cols(c):
            return xs_first[c][:]

        def gather_bytes(c):
            xs_first[c] = held([P, 4 * TILE], U8, f"xs_first{c}", BYTE_TAGS[c])
            nc.vector.tensor_copy(byte_cols(c), xs_win[:].indirect(slots(c * 4 * TILE, (c + 1) * 4 * TILE)))

        def move_bytes(c):
            nc.sync.dma_start(out=xs_second[c][0:112, :].bitcast(I32), in_=byte_cols(c)[16:P, :].bitcast(I32))

        def load_tokens(o):
            nc.sync.dma_start(out=xw_win[o][:], in_=x_words[o].rearrange("p t r -> p (t r)").bitcast(I32))

        def word_col(g, o):
            return WORD_TILES[o][g] * TILE

        def gather_words(o, g0, g1):
            window = xw_win[o][:].bitcast(U32)
            col = word_col(g0, o)
            nc.vector.tensor_copy(
                xg[:, col : col + (g1 - g0) * TILE], window.indirect(slots(g0 * TILE, g1 * TILE))
            )

        def token_scales(e, o, j):
            c, place = divmod(2 * e + j, 4)
            return (xs_first[c], xs_second[c])[o][:, place * TILE : (place + 1) * TILE]

        def up_pass(g, m, o):
            e, j = divmod(g, 2)
            grp = group_of(SCALE_GROUPS, e)
            col = ((e - SCALE_GROUPS[grp][0]) * PASSES + o) * H
            nc.tensor.matmul_mx(
                out=up_bank(g, m)[:],
                lhsT=xg[:, word_col(g, o) : word_col(g, o) + TILE].bitcast(FP8X4),
                lhsT_scale=token_scales(e, o, j),
                rhs=weights(e, m, o).bitcast(FP4X4),
                rhs_scale=(w1_pl, w3_pl)[m][grp][:, col : col + H],
                start=(o == 0),
                stop=(o == PASSES - 1),
            )

        def by_word_half(bank):
            return bank[:].rearrange("s (p u d) -> s u p d", u=2, d=2)

        h_tiles = {}

        def gated(g):
            act = held([P, H], F32, f"act{g}")
            nc.scalar.activation(
                act[:].rearrange("s (u p d) -> s u p d", u=2, d=2), by_word_half(up_bank(g, 0)), SILU
            )
            h = held([P, H], BF16, f"h{g}")
            if g < SHARED:
                lin = held([P, H], F32, f"lin{g}")
                nc.scalar.copy(lin[:].rearrange("s (u p d) -> s u p d", u=2, d=2), by_word_half(up_bank(g, 1)))
                nc.gpsimd.tensor_tensor(h[:], lin[:], act[:], MULT)
            elif g == TILES - 1:
                for u in range(2):
                    nc.vector.tensor_tensor(
                        h[:].rearrange("s (u p d) -> s u p d", u=2, d=2)[:, u],
                        by_word_half(up_bank(g, 1))[:, u],
                        act[:].rearrange("s (u p d) -> s u p d", u=2, d=2)[:, u],
                        MULT,
                    )
            else:
                nc.vector.tensor_tensor(
                    h[:].rearrange("s (u p d) -> s u p d", u=2, d=2),
                    by_word_half(up_bank(g, 1)),
                    act[:].rearrange("s (u p d) -> s u p d", u=2, d=2),
                    MULT,
                )
            h_tiles[g] = h

        packed = {}

        turned = {}

        def turn(tiles, bank, copy_out=nc.scalar.copy):
            width = len(tiles) * TILE
            for j, g in enumerate(tiles):
                words = h_tiles[g][:].bitcast(F32)
                for u in range(2):
                    col = (2 * j + u) * TILE
                    nc.tensor.transpose(bank[:, col : col + TILE], words[:, u * P : (u + 1) * P], ident[:])
            h_turned = held([P, 4 * width], BF16, f"h_turned{tiles[0]}")
            copy_out(
                h_turned[:].bitcast(F32).rearrange("p (j s u) -> p j s u", u=2, s=TILE),
                bank[:, : 2 * width].rearrange("p (j u s) -> p j s u", u=2, s=TILE),
            )
            turned[tiles[0]] = (h_turned, width)

        def quantize(first):
            h_turned, width = turned[first]
            codes = held([P, width], U32, f"codes{first}")
            h_scales = held([P, width], U8, f"h_scales{first}")
            nc.vector.quantize_mx(out=codes[:].bitcast(FP8X4), scales=h_scales[:], in_=h_turned[:])
            packed[first] = (codes, h_scales, width)

        def down(firsts, bank, copy_out):
            col = 0
            for g in firsts:
                codes, h_scales, width = packed[g]
                e = g // 2
                nc.tensor.matmul_mx(
                    out=bank[:, col : col + width],
                    lhsT=w2_sb[:, e * 2 * N : (e + 1) * 2 * N].bitcast(FP4X4),
                    lhsT_scale=w2_pl[:, e * N : (e + 1) * N],
                    rhs=codes[:].bitcast(FP8X4),
                    rhs_scale=h_scales[:],
                    start=True,
                    stop=True,
                )
                col = col + width
            copy_out(y_sb[:, firsts[0] * TILE : firsts[0] * TILE + col], bank[:, :col])

        gather_bytes(0)
        load_tokens(0)
        load_lead(0)
        load_plane(nc.scalar, w1_pl[0], w1_scales, *SCALE_GROUPS[0], range(1))
        load_plane(nc.sync, w1_pl[0], w1_scales, *SCALE_GROUPS[0], range(1, 4))
        load_tokens(1)
        load_lead(1)
        load_words(1, 0)
        load_plane(nc.sync, w3_pl[0], w3_scales, *SCALE_GROUPS[0], range(2))
        load_pair()
        move_bytes(0)
        load_words(1, 1)
        zero(nc.gpsimd, w2_pl[:])
        load_plane(nc.gpsimd, w3_pl[0], w3_scales, *SCALE_GROUPS[0], range(2, 4))
        make_identity(nc, ident[:])
        load_scales(nc.sync, 0, 1)
        load_words(1, 2)
        load_words(0, 2)

        gather_words(0, 0, 1)
        gather_words(0, 1, 2)
        gather_words(0, 2, 4)
        gather_words(1, 0, 2)
        gather_words(1, 2, 4)
        for g in range(SHARED):
            up_pass(g, 0, 0)
        load_scales(nc.sync, 1, 1)
        gather_bytes(1)
        move_bytes(1)
        for m, o in ((1, 0), (0, 1), (1, 1)):
            for g in (0, 1):
                up_pass(g, m, o)
        for g in (2, 3):
            up_pass(g, 0, 1)
        for g in (2, 3):
            for o in range(PASSES):
                up_pass(g, 1, o)
        gather_words(0, 4, 8)
        gather_words(1, 4, 8)
        gather_bytes(2)
        for o in range(PASSES):
            gather_words(o, 8, 10)
        load_words(1, 3)
        load_words(0, 3)
        load_scales(nc.sync, 0, 2)
        load_words(1, 4)
        load_words(0, 4)
        load_scales(nc.sync, 1, 2)

        for g in range(SHARED):
            gated(g)

        for g in range(SHARED, TILES - 2):
            if g in (4, 8):
                for m in range(2):
                    for tile in (g, g + 1):
                        up_pass(tile, m, 0)
                if g == 4:
                    for tile in (g, g + 1):
                        for m in range(2):
                            up_pass(tile, m, 1)
                else:
                    for m in range(2):
                        for tile in (g, g + 1):
                            up_pass(tile, m, 1)
            elif g not in (5, 9):
                for m in range(2):
                    for o in range(PASSES):
                        up_pass(g, m, o)
            if g == 4:
                move_bytes(2)
                load_words(1, 5)
                load_words(0, 5)
                load_plane(nc.sync, w2_pl, w2_scales, 0, E)
                nc.sync.dma_start(
                    out=w2_sb[:].bitcast(I32).rearrange("p (e b) -> p e b", e=E),
                    in_=w2_words.rearrange("e s p b -> p (e s) b").bitcast(I32),
                )
                nc.sync.dma_start(pos1_sb[:], pos1)
                nc.sync.dma_start(pos2_sb[:], pos2)
                nc.sync.dma_start(out=gate_sb[:], in_=gate.rearrange("r n t -> n r t"))
            gated(g)
            if g in (6, 7):
                gather_words(g - 6, 10, 12)
            if g == 9:
                turn([0, 1], up_bank(8, 0))
                turn([2, 3], up_bank(9, 0), nc.vector.tensor_copy)
                turn([4, 5], up_bank(8, 1))
                turn([6, 7], up_bank(9, 1))
                for first in (0, 2, 4, 6):
                    quantize(first)

        for m in range(2):
            for g in (10, 11):
                for o in range(PASSES):
                    up_pass(g, m, o)
        gated(10)
        gated(11)
        turn([8, 9], up_bank(10, 0))
        turn([10], up_bank(9, 0), nc.vector.tensor_copy)
        turn([11], up_bank(8, 0))
        for first in (8, 10, 11):
            quantize(first)
        down([0, 2], up_bank(11, 1), nc.scalar.copy)
        down([4, 6], up_bank(10, 1), nc.scalar.copy)
        down([8], up_bank(9, 1), nc.vector.tensor_copy)
        down([10], up_bank(8, 1), nc.vector.tensor_copy)
        down([11], up_bank(11, 0), nc.vector.tensor_copy)

        def chosen(r, lo, hi):
            return y_sb[:].indirect((pos1_sb, pos2_sb)[r][:, lo // LIST : hi // LIST])

        split = PIECES[0][1]
        firsts = held([P, T - split], F32, "firsts")
        nc.vector.tensor_tensor(firsts[:], chosen(0, split, T), gate_sb[:, 0, split:T], MULT)
        both = held([P, 2, split], F32, "both")
        for r in range(2):
            nc.scalar.activation(both[:, r, :], chosen(r, 0, split), COPY)
        plain = [both]
        for lo, hi in PIECES[1:]:
            plain.append(held([P, hi - lo], F32, f"plain{lo}"))
            nc.scalar.activation(plain[-1][:], chosen(1, lo, hi), COPY)

        weighted = []

        def weigh(i):
            lo, hi = PIECES[i]
            weighted.append(held(plain[i].shape, F32, f"weighted{lo}"))
            factor = gate_sb[:, :, lo:hi] if i == 0 else gate_sb[:, 1, lo:hi]
            nc.vector.tensor_tensor(weighted[i][:], plain[i][:], factor, MULT)

        def finish(i):
            lo, hi = PIECES[i]
            total = held([P, hi - lo], F32, f"total{lo}")
            if i == 0:
                nc.vector.tensor_tensor(total[:], weighted[i][:, 0, :], weighted[i][:, 1, :], ADD)
            else:
                nc.vector.tensor_tensor(total[:], firsts[:, lo - split : hi - split], weighted[i][:], ADD)
            nc.sync.dma_start(out=out[:, lo:hi], in_=total[:])

        for i in range(0, len(PIECES), 2):
            weigh(i)
            weigh(i + 1)
            finish(i)
            finish(i + 1)
